import numpy as np, ml_dtypes
CORES = [66,74,82,90,194,202,210,218]
N = 8
import mx_ref
BF = ml_dtypes.bfloat16
def gcols(t, e):
    v = np.concatenate([t.reshape(8, 16, -1, 4), np.zeros((8, 16, 1, 4), BF)], axis=2)
    return np.ascontiguousarray(np.stack([v[g][:, e[g]] for g in range(8)])).reshape(128, -1)
def cut(t, i, w=512):
    return t[:, w * i:w * i + w]
def pick(q, e):
    c = np.concatenate([q[0].reshape(128, -1, 4), np.zeros((128, 1, 4), np.uint8)], axis=1); s = np.concatenate([q[1], np.ones((16, 1), np.uint8)], axis=1)
    return (np.ascontiguousarray(c[:, e].reshape(128, -1)), np.ascontiguousarray(s[:, e]))
def join(*qs):
    return (np.concatenate([q[0] for q in qs], axis=1), np.concatenate([q[1] for q in qs], axis=1))
def put(q, e, v):
    c, s = q[0].reshape(128, -1, 4).copy(), q[1].copy(); c[:, e] = v[0].reshape(128, -1, 4); s[:, e] = v[1]
    return (c.reshape(128, -1), s)
def pk(c, s):
    return (np.ascontiguousarray(c), mx_ref.live(s))
def emit(q):
    return q[0], q[1]
def packed(v, rng):
    q = [mx_ref.quantize(np.ascontiguousarray(v[r])) for r in range(N)]
    return np.stack([a for a, b in q]), np.stack([mx_ref.plane(b, rng) for a, b in q])
def values_of_codes():
    e, c = np.zeros((128, 128, 4), np.float32), np.zeros((128, 2, 4), np.uint8)
    e[np.arange(128), np.arange(128), 0] = 1
    c[:127, :, 0] = np.arange(256).reshape(2, 128).T[:127]
    return mx_ref.matmul(mx_ref.quantize(e.reshape(128, 512).astype(BF)), (c.reshape(128, 8), np.full((16, 2), 127, np.uint8))).T.reshape(-1).astype(np.float64)
CODE_VALUE, SCALE_VALUE = values_of_codes(), 2.0 ** (np.arange(256) - 127.0)
def decode(q):
    return (CODE_VALUE[q[0]].reshape(16, 8, -1, 4) * SCALE_VALUE[q[1]][:, None, :, None] + 0.0).reshape(128, -1).astype(np.float32)
def f(rng, *shape):
    return mx_ref.flush((rng.standard_normal(shape, dtype=np.float32) * np.exp2(rng.integers(-2, 3, shape[:-1] + (1,)))).astype(BF))
def wide(rng, *shape, cols=0):
    v = rng.standard_normal(shape, dtype=np.float32) * np.exp2(rng.integers(-12, 13, shape)).astype(np.float32)
    if cols: v *= np.repeat(np.exp2(rng.integers(-cols, cols + 1, shape[:-2] + (1, shape[-1] // 4))) * (rng.random(shape[:-2] + (1, shape[-1] // 4)) > 0.0625), 4, axis=-1).astype(np.float32)
    return mx_ref.flush(v.astype(BF))
C, M, L, T = 256, 512, 9, 3
def two(i):
    return np.arange(2 * C * i, 2 * C * i + 2 * C)
def product(a, q):
    return np.concatenate([mx_ref.matmul(a, pick(q, two(i))) for i in range(N // 2)], axis=1)
def unpacked(q):
    return np.concatenate([decode(pick(q, two(i))) for i in range(N // 2)], axis=1)
def place(a):
    e = np.full((8, M), C)
    np.minimum.at(e, (np.arange(8)[:, None], a), np.arange(C)[None, :])
    return np.where(e < C, M + e, np.arange(M)[None, :])
def same(a):
    return np.stack([a] * N)
def weights(rng, w):
    c, p = packed(same(w), rng)
    return {"wc": c, "ws": p}
def numbers_of(rng):
    return {"x": np.array(f(rng, N, 128, 4 * C)), "m": np.array(f(rng, N, 128, 4 * M))}
def digits(e, size):
    v = np.zeros(e.shape + (32,))
    v[..., :L] = (((e[..., None] >> np.arange(L)) & 1) * 2 - 1) * size[None, :, None, None]
    return np.moveaxis(v.reshape(e.shape + (8, 4)), 2, 3).astype(np.float32).astype(BF)
def setup_inputs(rng):
    return {**numbers_of(rng), "u": same(f(rng, 128, 512)), **weights(rng, f(rng, 128, 2048))}
def setup_inputs_ties(rng):
    d = numbers_of(rng)
    e = rng.permutation(N)
    x = d["x"].reshape(N, 8, 16, C, 4)
    for r in range(N):
        k = rng.permutation(C)
        if r == e[0]: k = np.zeros(C, int)
        elif r == e[2]: k = np.where(k < 256, 0, 2)
        else: k = k % 3
        a = x[r][:, :8, :3].copy()
        a[:, :, 2] = 0
        x[r][:, :8] = a[:, :, k]
    x[e[1]] = 0
    u = np.array(f(rng, 128, 512)).reshape(8, 16, 128, 4)
    u[:, 8:] = 0
    w = np.array(f(rng, 128, 2048)).reshape(8, 16, 4, 8, 16, 4)
    w[:, 8:, :, :, :8] = 0
    return {"x": x.reshape(N, 128, 4 * C), "m": d["m"], "u": same(u.reshape(128, 512)), **weights(rng, w.reshape(128, 2048))}
def setup_inputs_crowd(rng):
    d = numbers_of(rng)
    for n in ("x", "m"):
        p = d[n].reshape(N, 128, -1, 4)
        p[:, 15] = 0
        p[:, 15, :, 0] = 1
        d[n] = p.reshape(N, 128, -1)
    u = np.array(f(rng, 128, 512)).reshape(128, 128, 4)
    k = rng.permutation(np.array([0, 0, 1, 2, 3, 5, 7, L]))
    h = np.flatnonzero(k == 0)
    for g in range(8):
        z = 16 * g + rng.permutation(L)[k[g]:]
        s = rng.integers(-1, 2, len(z)) if k[g] else np.full(len(z), int(g == h[0]))
        u[:, z] = 0
        u[15, z, 0] = s.astype(np.float32).astype(BF)
    w = np.array(f(rng, 128, 2048)).reshape(128, 4, 128, 4)
    w[:, :, 15] = 0
    return {**d, "u": same(u.reshape(128, 512)), **weights(rng, w.reshape(128, 2048))}
def setup_inputs_chain(rng):
    d = numbers_of(rng)
    s = rng.permutation(8) % 2 * 2 - 1
    size = np.where(s > 0, 2.0 ** 28, 2.0 ** -30)
    x, m = d["x"].reshape(N, 8, 16, C, 4), d["m"].reshape(N, 8, 16, M, 4)
    to = np.stack([[rng.permutation(M) for g in range(8)] for r in range(N)])
    at = np.stack([[rng.permutation(M)[:C] for g in range(8)] for r in range(N)])
    x[:, :, :8] = digits(at, size)
    m[:, :, :8] = digits(to, size)
    u = np.array(f(rng, 128, 512)).reshape(8, 16, 128, 4)
    for g in range(8):
        for i in range(L):
            u[:, :, 16 * g + i] = 0
            u[g, i // 4, 16 * g + i, i % 4] = 2.0 ** 30 if s[g] > 0 else 2.0 ** -30
    w = np.array(f(rng, 128, 2048)).reshape(8, 16, 4, 8, 16, 4)
    w[:, :8] = 0
    w[:, :, :, :, :8] = 0
    for g in rng.permutation(8)[:4]:
        z = (N, 8, M, 4)
        m[:, g, 8:] = (rng.integers(8, 16, z) * np.exp2(-1.0 * rng.integers(13, 22, z)) * rng.choice([-1.0, 1.0], z)).astype(np.float32).astype(BF)
        m[:, g, 8, :, 0] = 1.625
        x[:, g, 8, :, 0] = -0.6875
        w[:, :, :, g, 8:] = 0
        w[g, 8, 0, g, 8, 0] = -32
    return {"x": x.reshape(N, 128, 4 * C), "m": m.reshape(N, 128, 4 * M), "u": same(u.reshape(128, 512)), **weights(rng, w.reshape(128, 2048))}
def setup_inputs_spread(rng):
    d = setup_inputs(rng)
    d["x"] = wide(rng, N, 128, 4 * C, cols=6)
    d["m"] = wide(rng, N, 128, 4 * M, cols=6)
    return d
def check_inputs(d):
    b = []
    for k in ("x", "m", "u"):
        a = np.abs(d[k].astype(np.float32))
        if not (np.isfinite(a).all() and ((a == 0) | (a >= 2.0 ** -30) & (a <= 2.0 ** 30)).all()): b.append("a value of " + k)
    if (d["u"].astype(np.float32) != d["u"][:1].astype(np.float32)).any(): b.append("u differs between ranks")
    if (d["wc"] != d["wc"][:1]).any(): b.append("wc differs between ranks")
    s = [mx_ref.live(p) for p in d["ws"]]
    if any((p != s[0]).any() for p in s): b.append("ws differs between ranks")
    a = np.abs(decode(pk(d["wc"][0], d["ws"][0])))
    if ((d["wc"] & 127) == 127).any() or not ((a == 0) | (a >= 2.0 ** -30) & (a <= 2.0 ** 30)).all(): b.append("a value of W")
    return b
def reference(x, m, u, wc, ws):
    w, qu = pk(wc[0], ws[0]), mx_ref.quantize(u[0])
    part = [pick(w, np.arange(128 * b, 128 * b + 128)) for b in range(4)]
    state = join(*[mx_ref.quantize(x[r]) for r in range(N)])
    maps = [m[r] for r in range(N)]
    power = (1 << np.arange(L)).reshape(1, L, 1, 1)
    for t in range(T):
        a = product(qu, state).reshape(8, 16, N, C)
        at = np.sum((a[:, :L] > 0) * power, axis=1)
        reads = np.concatenate([gcols(maps[(r + t) % N], at[:, r]) for r in range(N)], axis=1)
        layer = np.stack([product(part[b], state) * np.float32(0.015625) for b in range(4)], axis=2).reshape(128, -1)
        state = mx_ref.quantize((layer + unpacked(mx_ref.quantize(reads))).astype(BF))
        new = unpacked(state).astype(BF)
        for r in range(N):
            h = (r + t) % N
            maps[h] = gcols(np.concatenate([maps[h], cut(new, r, 4 * C)], axis=1), place(at[:, r]))
    last = product(part[0], state)
    y = np.zeros((N, 128, C), np.float32)
    oc, osc = np.zeros((N, 128, 4 * (C + M)), np.uint8), np.zeros((N, 16, C + M), np.uint8)
    for r in range(N):
        y[r] = cut(last, r, C)
        oc[r], osc[r] = emit(join(pick(state, C * r + np.arange(C)), mx_ref.quantize(maps[r])))
    return {"y": y, "oc": oc, "osc": osc}

@@ -1,0 +1,340 @@
+from concourse.mybir import dt, AluOpType as Alu, AxisListType, ActivationFunctionType as Act
+
+C, M, VISITS = 256, 512, 3
+X4, U8, BF, F32, U16, I32 = "float8_e4m3fn_x4", "uint8", "bfloat16", "float32", "uint16", "int32"
+BIG, BASE = 16384.0, 4194304.0
+SHIFTS = 8
+EARLY = 5
+SPLIT = 70
+LAST = 40
+
+
+def _sb(n, d):
+    return ("sbuf", [128, n], d)
+
+
+SCRATCH = {
+    "xt": _sb(4 * C, BF), "ut": _sb(512, BF), "pool": _sb(4 * M + VISITS * 4 * C, BF),
+    "wq": _sb(512, X4), "wsq": _sb(512, U8), "uq": _sb(128, X4), "usq": _sb(128, U8),
+    "l0c": _sb(C, X4), "l0s": _sb(C, U8), "l1c": _sb(C, X4), "l1s": _sb(C, U8), "l2c": _sb(C, X4), "l2s": _sb(C, U8),
+    "l3c": _sb(C, X4), "fins": _sb(C + M, U8), "qmc": _sb(M, X4),
+    "y0c": _sb(C, X4), "y0s": _sb(C, U8), "y1c": _sb(C, X4), "y1s": _sb(C, U8), "y2c": _sb(C, X4), "y2s": _sb(C, U8),
+    "bits": _sb(512, BF), "bitq": _sb(128, X4), "bitss": _sb(128, U8),
+    "off": _sb(64, U16), "own": _sb(64, F32), "bt": _sb(4 * C, BF), "bq": _sb(C, X4), "bs": _sb(C, U8), "yt": _sb(4 * C, BF),
+    "fl": _sb(768, BF), "flq": _sb(192, X4), "fls": _sb(192, U8),
+    "v2": _sb(64, F32), "o16": _sb(16, U16),
+    "tab": _sb(M + 256, F32), "val": _sb(VISITS * C, F32), "scan": _sb(M, F32), "moff": _sb(128, U16),
+    "mc1": _sb(4 * M, BF), "mc2": _sb(4 * M, BF), "mc3": _sb(4 * M, BF),
+    "zero": _sb(1024, BF), "c64": _sb(128, BF), "ident": _sb(128, BF), "et": _sb(2048, BF), "eq": _sb(512, X4), "es": _sb(512, U8),
+    "kt": _sb(2048, BF), "kq": _sb(512, X4), "ks": _sb(512, U8),
+    "iq": _sb(1, I32), "ci": _sb(8, I32), "cf": _sb(8, F32), "col": _sb(8, F32), "i18": _sb(18, F32), "t18": _sb(18, F32),
+    "ia": _sb(128, BF), "ic": _sb(128, BF), "i4": _sb(M, BF), "t4": _sb(4, F32),
+    "spare": _sb(2, F32), "kscan": _sb(M, BF), "ysb": _sb(C, F32),
+    "pa": ("psum", [128, 512], F32), "po": ("psum", [128, 512], F32), "pc": ("psum", [128, 512], F32), "ps": ("psum", [128, 512], F32),
+    "pr0": ("psum", [128, 512], F32), "pr1": ("psum", [128, 512], F32), "pr2": ("psum", [128, 512], F32), "pr3": ("psum", [128, 512], F32),
+}
+DMAS = ["dx", "du", "dm", "dws", "dwa", "dwb", "dy", "dsc", "dma", "dmb", "ds0", "ds1", "ds2", "ds3"]
+SEMAPHORES = ["qv", "qs", "qt", "qg", "arr1", "arr2", "arr3", "arr3c", "sent"] + DMAS
+PSUM = ("pa", "po", "pc", "ps", "pr0", "pr1", "pr2", "pr3")
+
+
+def rank_program(g, core, T, topo):
+    rank = T.rank_of(core)
+    if rank is None:
+        return
+    n = len(T.cores)
+    eng = {"v": g.vector, "s": g.scalar, "t": g.tensor, "g": g, "y": g.sync}
+    counter = {"v": "qv", "s": "qs", "t": "qt", "g": "qg"}
+    ops, writer, readers, bank = [], {}, {}, {}
+
+    def op(q, fn, reads=(), writes=(), dma=None, after=()):
+        me = len(ops)
+        deps = set()
+        for k in reads:
+            if k not in PSUM and k in writer:
+                deps.add(writer[k])
+        for k in writes:
+            if k in PSUM:
+                continue
+            for d in [writer.get(k)] + readers.get(k, []):
+                if d is not None:
+                    deps.add(d)
+        for k in list(reads) + list(writes):
+            if k in PSUM:
+                for q2, d in bank.setdefault(k, {}).items():
+                    if q2 != q:
+                        deps.add(d)
+                bank[k][q] = me
+        for k in reads:
+            readers.setdefault(k, []).append(me)
+        for k in writes:
+            writer[k] = me
+            readers[k] = []
+        ops.append({"q": q, "fn": fn, "deps": deps, "dma": dma, "after": list(after), "need": False})
+
+    def V(fn, r=(), w=(), **k):
+        op("v", fn, r, w, **k)
+
+    def S(fn, r=(), w=(), **k):
+        op("s", fn, r, w, **k)
+
+    def P(fn, r=(), w=(), **k):
+        op("t", fn, r, w, **k)
+
+    def G(fn, r=(), w=(), **k):
+        op("g", fn, r, w, **k)
+
+    v, s, pe = g.vector, g.scalar, g.tensor
+
+    def ts(out, in0, a, b, o0, o1=None):
+        if o1 is None:
+            return lambda: v.tensor_scalar(out, in0, a, None, o0)
+        return lambda: v.tensor_scalar(out, in0, a, b, o0, o1)
+
+    def mm(out, w, ws, x, xs, start, stop):
+        return lambda: pe.matmul_mx(out, w, ws, x, xs, start, stop)
+
+    def qz(c, sc, t):
+        return lambda: v.quantize_mx(c, sc, t)
+
+    def iota(out, pattern, base, cm, small=True):
+        if small:
+            return lambda: g.iota(out, pattern, base, cm, allow_small_or_imprecise_dtypes=True)
+        return lambda: g.iota(out, pattern, base, cm)
+
+    def act(out, in_, scale=None):
+        if scale is None:
+            return lambda: s.activation(out, in_, Act.Copy)
+        return lambda: s.activation(out, in_, Act.Copy, scale=scale)
+
+    def load(q, out, in_, reads, writes, sem, after=()):
+        op(q, lambda: eng[q].dma_start(out, in_), reads, writes, dma=sem, after=after)
+
+    load("y", T.xt[:], T.x[:], (), ["xt"], "dx")
+    load("s", T.ut[:], T.u[:], (), ["ut"], "du")
+    load("y", T.pool[:, 0:4 * M], T.m[:], (), ["pool_m"], "dm")
+    load("y", T.wsq[:], T.ws[:], (), ["ws"], "dws")
+    load("y", T.wq[:, 0:256].bitcast(dt.uint8), T.wc[:, 0:1024], (), ["w0", "w1"], "dwa")
+    load("y", T.wq[:, 256:512].bitcast(dt.uint8), T.wc[:, 1024:2048], (), ["w2", "w3"], "dwb")
+
+    G(iota(T.iq[:], [[0, 1]], 0, 1, False), (), ["iq"])
+    G(iota(T.i18[:], [[1, 18]], -2, 0), (), ["i18"])
+    G(iota(T.ia[:], [[4, 8], [1, 4], [0, 4]], 0, 0), (), ["ia"])
+    G(iota(T.ic[:], [[4, 8], [0, 4], [1, 4]], 0, 0), (), ["ic"])
+    V(lambda: v.memset(T.c64[:], 64.0), (), ["c64"])
+    V(lambda: v.memset(T.zero[:], 0.0), (), ["zero"])
+    G(lambda: g.affine_select(T.ident[:], T.c64[:], [[-1, 128]], Alu.is_equal, 0.0, 0, 1), ["c64"], ["ident"])
+    G(iota(T.tab[:, 0:M], [[4, M]], 0, 0), (), ["tab"])
+    G(iota(T.i4[:], [[0, M // 4], [1, 4]], 0, 0), (), ["i4"])
+    G(iota(T.spare[:], [[128, 2]], M, 1), (), ["spare"])
+    V(ts(T.ci[:, 0:1], T.iq[:], 2, None, Alu.logical_shift_right), ["iq"], ["ci0"])
+    V(ts(T.ci[:, 1:2], T.iq[:], 2, 28, Alu.logical_shift_right, Alu.bitwise_and), ["iq"], ["ci1"])
+    V(ts(T.ci[:, 2:3], T.iq[:], 2, 3, Alu.logical_shift_right, Alu.bitwise_and), ["iq"], ["ci2"])
+    V(ts(T.ci[:, 3:4], T.iq[:], 3, None, Alu.bitwise_and), ["iq"], ["ci3"])
+    V(ts(T.ci[:, 4:5], T.iq[:], 15, None, Alu.bitwise_and), ["iq"], ["ci4"])
+    V(lambda: v.memset(T.bits[:, C:512], 0.0), (), ["bitpad"])
+    V(lambda: v.tensor_copy(T.cf[:, 0:5], T.ci[:, 0:5]), ["ci0", "ci1", "ci2", "ci3", "ci4"], ["cf"])
+    q4, g4, tau, bcol, icol = [T.cf[:, j:j + 1] for j in range(5)]
+    p2, pw, lt, scol, scol4 = [T.col[:, j:j + 1] for j in range(5)]
+    V(ts(T.t18[:], T.i18[:], icol, 1.0, Alu.is_lt, Alu.add), ["i18", "cf"], ["t18"])
+    for t in range(4):
+        V(ts(T.kt[:, t:512:4], T.ia[:], float(t), g4, Alu.subtract, Alu.is_equal), ["ia", "cf"], ["ka%d" % t])
+    V(lambda: v.tensor_reduce(p2, T.t18[:], AxisListType.X, Alu.mult), ["t18"], ["p2"])
+    for t in range(4):
+        V(ts(T.kt[:, 512 + t:1024:4], T.ic[:], float(t), g4, Alu.subtract, Alu.is_equal), ["ic", "cf"], ["kc%d" % t])
+    V(ts(pw, icol, 9.0, p2, Alu.is_lt, Alu.mult), ["cf", "p2"], ["pw"])
+    V(qz(T.kq[:, 0:256], T.ks[:, 0:256], T.kt[:, 0:1024]), ["ka%d" % t for t in range(4)] + ["kc%d" % t for t in range(4)], ["kq0"])
+    V(lambda: v.memset(T.fl[:], 0.0), (), ["fl%d" % j for j in range(SHIFTS)])
+    S(act(T.et[:, 0:1024], T.zero[:]), ["zero"], ["e0", "e1"])
+    S(act(T.et[:, 1024:2048], T.zero[:]), ["zero"], ["e2", "e3"])
+    for b in range(4):
+        S(act(T.et[:, 512 * b + b:512 * b + 512:4], T.ident[:]), ["ident"], ["e%d" % b])
+    S(lambda: s.activation(T.val[:, 0:M], T.tab[:, 0:M], Act.Identity, bias=float(4 * M)), ["tab"], ["val0"])
+    S(lambda: s.activation(T.val[:, M:M + C], T.tab[:, 0:C], Act.Identity, bias=float(8 * M)), ["tab"], ["val1"])
+
+    def late_constants():
+        V(ts(lt, bcol, tau, BIG, Alu.is_lt, Alu.mult), ["cf"], ["lt"])
+        V(ts(T.t4[:], T.i4[:, 0:4], tau, 1.0 / BASE, Alu.is_le, Alu.max), ["i4", "cf"], ["t4"])
+        for t in range(1, 8):
+            V(ts(T.kt[:, 1024 + 512 * (t // 4) + t % 4:1536 + 512 * (t // 4):4], T.ic[:], q4, BIG, Alu.is_equal, Alu.mult), ["ic", "cf"], ["kd%d" % t])
+        V(ts(T.kt[:, 1024:1536:4], T.ic[:], q4, lt, Alu.is_equal, Alu.mult), ["ic", "cf", "lt"], ["kd0"])
+        V(lambda: v.tensor_reduce(scol, T.t4[:], AxisListType.X, Alu.mult), ["t4"], ["scol"])
+        V(qz(T.kq[:, 256:512], T.ks[:, 256:512], T.kt[:, 1024:2048]), ["kd%d" % t for t in range(8)], ["kq1"])
+        V(ts(T.kscan[:], T.i4[:], tau, BASE, Alu.is_gt, Alu.mult), ["i4", "cf"], ["kscan"])
+        V(ts(scol4, scol, 0.25, None, Alu.mult), ["scol"], ["scol4"])
+
+    V(qz(T.uq[:], T.usq[:], T.ut[:]), ["ut"], ["uq"])
+    V(qz(T.l0c[:], T.l0s[:], T.xt[:]), ["xt"], ["state0"])
+
+    banks = [T.pr0, T.pr1, T.pr2, T.pr3]
+    engines = [0]
+
+    def kside(j):
+        return T.kq[:, 128 * j:128 * j + 128], T.ks[:, 128 * j:128 * j + 128]
+
+    def wside(b):
+        return T.wq[:, 128 * b:128 * b + 128], T.wsq[:, 128 * b:128 * b + 128]
+
+    def eside(b):
+        return T.eq[:, 128 * b:128 * b + 128], T.es[:, 128 * b:128 * b + 128]
+
+    def map_offsets(a, z, key):
+        V(lambda: v.tensor_tensor_scan(T.scan[:, 4 * a:4 * z], T.kscan[:, 4 * a:4 * z], T.tab[:, 4 * a:4 * z], 0.0, Alu.mult, Alu.add),
+          ["kscan", "tab"], ["scan" + key])
+        V(ts(T.moff[:, a:z], T.scan[:, 4 * a + 3:4 * z:4], scol, bcol, Alu.mult, Alu.add), ["scan" + key, "scol", "cf"], ["moff" + key])
+
+    def gather(q, out, win, offs, reads, key):
+        if q == "v":
+            V(lambda: v.tensor_copy(out, win.indirect(offs)), reads, [key])
+        else:
+            S(lambda: s.activation(out, win.indirect(offs), Act.Copy), reads, [key])
+
+    def hop(out, in_, sem, dst, key):
+        rid, pid = topo.addr(dst, core)
+        engines[0] += len(topo.engines(core, dst))
+        G(lambda: g.remote_dma(out, in_, T.sem[sem], T.sem.sent, pid, rid, topo.mask(core, dst)), [key], dma="remote")
+
+    before = len(topo.engines(T.cores[(rank - 1) % n], core))
+    home = len(topo.engines(T.cores[(rank + VISITS - 1) % n], core))
+
+    for t in range(VISITS):
+        sc_, ss_ = T["l%dc" % t][:], T["l%ds" % t][:]
+        yc, ys = T["y%dc" % t], T["y%ds" % t]
+        st = ["state0"] if t == 0 else []
+        final = t + 1 == VISITS
+        win, wkey = (T.pool[:, 0:4 * M], ["pool_m"]) if t == 0 else (T["mc%d" % t][:], ["mc%da" % t, "mc%db" % t])
+        lo = 4 * M + 4 * C * t
+
+        def layer(b, start, stop):
+            P(mm(banks[b][:, 0:C], *wside(b), sc_, ss_, start, stop), st + ["w%d" % b, "ws"], ["pr%d" % b])
+
+        def unpack(b, c, sc2, key, start, stop):
+            P(mm(banks[b][:, 0:C], *eside(b), c, sc2, start, stop), [key, "eq"], ["pr%d" % b])
+
+        def compare(j):
+            h = j // 4
+            V(lambda: v.tensor_tensor(T.fl[:, 256 * h + 4 * j + j % 4:256 * h + 256:4], T.pc[:, 0:64 - j], T.own[:, j:64], Alu.is_equal),
+              ["pc", "own"], ["fl%d" % j])
+
+        def written(b):
+            unpack(b, yc[:], ys[:], "yq%d" % t, True, True)
+            S(act(T.pool[:, lo + b:lo + 4 * C:4], banks[b][:, 0:C], 0.015625), ["pr%d" % b], ["pool%d_%d" % (t, b)])
+
+        P(mm(T.pa[:, 0:C], T.uq[:], T.usq[:], sc_, ss_, True, True), st + ["uq"], ["pa"], after=[("arr%d" % t, 2 * before)] if t else [])
+        V(ts(T.bits[:, 0:C], T.pa[:, 0:C], 0.0, pw, Alu.is_gt, Alu.mult), ["pa", "pw"], ["bits"])
+        if t:
+            layer(0, True, False)
+            layer(1, True, False)
+        V(qz(T.bitq[:], T.bitss[:], T.bits[:]), ["bits", "bitpad"], ["bitq"])
+        P(mm(T.po[:, 0:128], *kside(0), T.bitq[:], T.bitss[:], True, True), ["kq0", "bitq"], ["po"])
+        P(mm(T.pc[:, 0:128], *kside(1), T.bitq[:], T.bitss[:], True, True), ["kq0", "bitq"], ["pc"])
+        V(ts(T.off[:], T.po[:, 0:64], bcol, None, Alu.add), ["po", "cf"], ["off"])
+        if t:
+            layer(2, True, False)
+            layer(3, True, False)
+        else:
+            V(qz(T.eq[:], T.es[:], T.et[:]), ["e0", "e1", "e2", "e3"], ["eq"])
+        gather("v", T.bt[:, 0:512], win, T.off[:, 0:32], wkey + ["off"], "bta")
+        gather("s", T.bt[:, 512:1024], win, T.off[:, 32:64], wkey + ["off"], "btb")
+        S(act(T.own[:], T.po[:, 0:64]), ["po"], ["own"])
+        V(qz(T.bq[:], T.bs[:], T.bt[:]), ["bta", "btb"], ["bq"])
+        if t == 0:
+            layer(0, True, False)
+            layer(1, True, False)
+        for b in range(4):
+            unpack(b, T.bq[:], T.bs[:], "bq", t == 0 and b > 1, t != 0 or b < 2)
+        if t == 0:
+            layer(2, False, True)
+            layer(3, False, True)
+        for j in range(EARLY):
+            compare(j)
+        for b in range(4):
+            if b % 2 == 0:
+                S(act(T.yt[:, b:4 * C:4], banks[b][:, 0:C], 0.015625), ["pr%d" % b], ["yt%d" % b])
+            else:
+                V(ts(T.yt[:, b:4 * C:4], banks[b][:, 0:C], 0.015625, None, Alu.mult), ["pr%d" % b], ["yt%d" % b])
+        V(qz(yc[:], ys[:], T.yt[:]), ["yt%d" % b for b in range(4)], ["yq%d" % t])
+        dst = T.cores[(rank - VISITS + 1) % n] if final else T.cores[(rank + 1) % n]
+        hop(T["l%dc" % (t + 1)][:].bitcast(dt.uint8), yc[:].bitcast(dt.uint8), "arr3c" if final else "arr%d" % (t + 1), dst, "yq%d" % t)
+        hop(T.fins[:, 0:C] if final else T["l%ds" % (t + 1)][:], ys[:], "arr%d" % (t + 1), dst, "yq%d" % t)
+        P(mm(T.ps[:, 0:128], *kside(1), T.bitq[:], T.bitss[:], True, False), ["kq0", "bitq"], ["ps"])
+        for b in range(3):
+            written(b)
+        for j in range(EARLY, SHIFTS):
+            compare(j)
+        V(qz(T.flq[:], T.fls[:], T.fl[:]), ["fl%d" % j for j in range(SHIFTS)], ["flq"])
+        if t == 0:
+            written(3)
+            late_constants()
+        P(mm(T.ps[:, 0:128], *kside(2), T.flq[:, 0:128], T.fls[:, 0:128], False, False), ["kq1", "flq"], ["ps"])
+        P(mm(T.ps[:, 0:128], *kside(3), T.flq[:, 64:192], T.fls[:, 64:192], False, True), ["kq1", "flq"], ["ps"])
+        if t:
+            written(3)
+        V(lambda: v.tensor_tensor_scan(T.v2[:], T.kscan[:, 0:64], T.ps[:, 0:64], 0.0, Alu.mult, Alu.add), ["kscan", "ps"], ["v2"])
+        for h in range(2):
+            V(ts(T.o16[:, h:16:2], T.v2[:, 3 + 4 * h:64:8], scol4, T.spare[:, h:h + 1], Alu.mult, Alu.min), ["v2", "scol4", "spare"], ["o16%d" % h])
+        for k in range(7, -1, -1):
+            V(lambda k=k, t=t: v.tensor_copy(T.tab[:].indirect(T.o16[:, 2 * k:2 * k + 2]), T.val[:, C * t + 32 * k:C * t + 32 * k + 32]),
+              ["o160", "o161", "val0", "val1"], ["tab"])
+        pk = ["pool_m"] + ["pool%d_%d" % (a, b) for a in range(t + 1) for b in range(4)]
+        mc, pwin = T["mc%d" % (t + 1)], T.pool[:, 0:lo + 4 * C]
+        if not final:
+            map_offsets(0, SPLIT, "a")
+            map_offsets(SPLIT, 128, "b")
+            gather("s", mc[:, 0:16 * SPLIT], pwin, T.moff[:, 0:SPLIT], pk + ["moffa"], "mc%da" % (t + 1))
+            gather("v", mc[:, 16 * SPLIT:4 * M], pwin, T.moff[:, SPLIT:128], pk + ["moffb"], "mc%db" % (t + 1))
+        else:
+            map_offsets(0, 64, "a")
+            map_offsets(64, 128, "b")
+            for a, key in ((0, "a"), (64, "b")):
+                gather("s", mc[:, 16 * a:16 * (a + LAST)], pwin, T.moff[:, a:a + LAST], pk + ["moff" + key], "ms" + key)
+                gather("v", mc[:, 16 * (a + LAST):16 * (a + 64)], pwin, T.moff[:, a + LAST:a + 64], pk + ["moff" + key], "mv" + key)
+                V(qz(T.qmc[:, 4 * a:4 * a + C], T.fins[:, C + 4 * a:2 * C + 4 * a], mc[:, 16 * a:16 * a + 4 * C]), ["ms" + key, "mv" + key], ["qm" + key])
+
+    codes, both = [("arr3c", home)], [("arr3c", home), ("arr3", home)]
+    P(mm(T.pa[:, 0:C], *wside(0), T.l3c[:], T.fins[:, 0:C], True, True), ["w0", "ws"], ["pa"], after=both)
+    load("y", T.oc[:, 4 * C:8 * C], T.qmc[:, 0:C].bitcast(dt.uint8), ["qma"], (), "dma")
+    load("y", T.oc[:, 0:4 * C], T.l3c[:].bitcast(dt.uint8), (), (), "dsc", after=codes)
+    load("y", T.oc[:, 8 * C:12 * C], T.qmc[:, C:2 * C].bitcast(dt.uint8), ["qmb"], (), "dmb")
+    S(act(T.ysb[:], T.pa[:, 0:C]), ["pa"], ["ysb"])
+    load("s", T.y[:], T.ysb[:], ["ysb"], (), "dy")
+    for k in range(4):
+        load("y" if k < 3 else "s", T.osc[4 * k:4 * k + 4, :], T.fins[32 * k:32 * k + 4, :], ["qma", "qmb"], (), "ds%d" % k, after=both[1:])
+
+    last = {}
+    for o in ops:
+        best = {}
+        for d in o["deps"]:
+            p = ops[d]
+            key = p["dma"] or p["q"]
+            best[key] = max(best.get(key, -1), d)
+        o["deps"] = []
+        for key, d in best.items():
+            if last.get((o["q"], key), -1) < d:
+                last[(o["q"], key)] = d
+                ops[d]["need"] = True
+                o["deps"].append(d)
+    count, seen = {}, set()
+    for o in ops:
+        q = o["q"]
+        for name, val in o["after"]:
+            if (q, name) not in seen:
+                seen.add((q, name))
+                eng[q].wait_ge(T.sem[name], val)
+        for d in o["deps"]:
+            eng[q].wait_ge(T.sem[ops[d]["sem"]], ops[d]["val"])
+        ins = o["fn"]()
+        if o["dma"] == "remote":
+            continue
+        if o["dma"]:
+            o["sem"], o["val"] = o["dma"], 16
+            ins.then_inc(T.sem[o["dma"]], 16)
+        elif o["need"]:
+            count[q] = count.get(q, 0) + 1
+            o["sem"], o["val"] = counter[q], count[q]
+            ins.then_inc(T.sem[counter[q]], 1)
+    g.wait_ge(T.sem.sent, engines[0])
+    for name in ("dma", "dsc", "dmb", "ds0", "ds1", "ds2"):
+        g.sync.wait_ge(T.sem[name], 16)
+    for name in ("dy", "ds3"):
+        s.wait_ge(T.sem[name], 16)

@@ -4,8 +4,6 @@ C, M, VISITS = 256, 512, 3
 X4, U8, BF, F32, U16, I32 = "float8_e4m3fn_x4", "uint8", "bfloat16", "float32", "uint16", "int32"
 BIG, BASE = 16384.0, 4194304.0
 SHIFTS = 8
-EARLY = 5
-SPLIT = 70
 LAST = 40
 
 
@@ -24,7 +22,9 @@ SCRATCH = {
     "fl": _sb(768, BF), "flq": _sb(192, X4), "fls": _sb(192, U8),
     "v2": _sb(64, F32), "o16": _sb(16, U16),
     "tab": _sb(M + 256, F32), "val": _sb(VISITS * C, F32), "scan": _sb(M, F32), "moff": _sb(128, U16),
-    "mc1": _sb(4 * M, BF), "mc2": _sb(4 * M, BF), "mc3": _sb(4 * M, BF),
+    "mc": _sb(4 * M, BF), "v1": _sb(64, F32), "r16": _sb(16, U16), "look": _sb(C, F32),
+    "dpool": _sb(4 * M + (VISITS - 1) * 4 * C, BF), "rt": _sb(4 * C, F32),
+    "mq": _sb(M, X4), "mqs": _sb(M, U8), "nq": _sb(C, X4), "nqs": _sb(C, U8),
     "zero": _sb(1024, BF), "c64": _sb(128, BF), "ident": _sb(128, BF), "et": _sb(2048, BF), "eq": _sb(512, X4), "es": _sb(512, U8),
     "kt": _sb(2048, BF), "kq": _sb(512, X4), "ks": _sb(512, U8),
     "iq": _sb(1, I32), "ci": _sb(8, I32), "cf": _sb(8, F32), "col": _sb(8, F32), "i18": _sb(18, F32), "t18": _sb(18, F32),
@@ -197,93 +197,136 @@ def rank_program(g, core, T, topo):
     before = len(topo.engines(T.cores[(rank - 1) % n], core))
     home = len(topo.engines(T.cores[(rank + VISITS - 1) % n], core))
 
+    H = C // 2
     for t in range(VISITS):
         sc_, ss_ = T["l%dc" % t][:], T["l%ds" % t][:]
         yc, ys = T["y%dc" % t], T["y%ds" % t]
         st = ["state0"] if t == 0 else []
         final = t + 1 == VISITS
-        win, wkey = (T.pool[:, 0:4 * M], ["pool_m"]) if t == 0 else (T["mc%d" % t][:], ["mc%da" % t, "mc%db" % t])
         lo = 4 * M + 4 * C * t
+        yq = ["yqa%d" % t, "yqb%d" % t]
+        dst = T.cores[(rank - VISITS + 1) % n] if final else T.cores[(rank + 1) % n]
+        land, csem = T["l%dc" % (t + 1)], "arr3c" if final else "arr%d" % (t + 1)
 
         def layer(b, start, stop):
             P(mm(banks[b][:, 0:C], *wside(b), sc_, ss_, start, stop), st + ["w%d" % b, "ws"], ["pr%d" % b])
 
-        def unpack(b, c, sc2, key, start, stop):
-            P(mm(banks[b][:, 0:C], *eside(b), c, sc2, start, stop), [key, "eq"], ["pr%d" % b])
+        def unpack(b, c, sc2, keys, start, stop):
+            P(mm(banks[b][:, 0:C], *eside(b), c, sc2, start, stop), keys + ["eq"], ["pr%d" % b])
 
         def compare(j):
             h = j // 4
             V(lambda: v.tensor_tensor(T.fl[:, 256 * h + 4 * j + j % 4:256 * h + 256:4], T.pc[:, 0:64 - j], T.own[:, j:64], Alu.is_equal),
               ["pc", "own"], ["fl%d" % j])
 
+        def pack_flags():
+            V(qz(T.flq[:], T.fls[:], T.fl[:]), ["fl%d" % j for j in range(SHIFTS)], ["flq"])
+
+        def flags():
+            P(mm(T.ps[:, 0:128], *kside(1), T.bitq[:], T.bitss[:], True, False), ["kq0", "bitq"], ["ps"])
+            P(mm(T.ps[:, 0:128], *kside(2), T.flq[:, 0:128], T.fls[:, 0:128], False, False), ["kq1", "flq"], ["ps"])
+            P(mm(T.ps[:, 0:128], *kside(3), T.flq[:, 64:192], T.fls[:, 64:192], False, True), ["kq1", "flq"], ["ps"])
+
         def written(b):
-            unpack(b, yc[:], ys[:], "yq%d" % t, True, True)
+            unpack(b, yc[:], ys[:], yq, True, True)
             S(act(T.pool[:, lo + b:lo + 4 * C:4], banks[b][:, 0:C], 0.015625), ["pr%d" % b], ["pool%d_%d" % (t, b)])
 
-        P(mm(T.pa[:, 0:C], T.uq[:], T.usq[:], sc_, ss_, True, True), st + ["uq"], ["pa"], after=[("arr%d" % t, 2 * before)] if t else [])
+        def pack_written():
+            V(qz(T.nq[:], T.nqs[:], T.pool[:, lo:lo + 4 * C]), ["pool%d_%d" % (t, b) for b in range(4)], ["nq"])
+
+        def rewritten(b):
+            unpack(b, T.nq[:], T.nqs[:], ["nq"], True, True)
+            S(act(T.dpool[:, lo + b:lo + 4 * C:4], banks[b][:, 0:C], 0.015625), ["pr%d" % b], ["dp%d_%d" % (t, b)])
+
+        def first_map(b):
+            name = ("pa", "po")[b % 2]
+            P(mm(T[name][:], *eside(b), T.mq[:], T.mqs[:], True, True), ["mq", "eq"], [name])
+            S(act(T.dpool[:, b:4 * M:4], T[name][:], 0.015625), [name], ["dpm%d" % b])
+
+        def scaled(b):
+            S(act(T.rt[:, b:4 * C:4], banks[b][:, 0:C], 0.015625), ["pr%d" % b], ["rt%d" % b])
+
+        P(mm(T.pa[:, 0:C], T.uq[:], T.usq[:], sc_, ss_, True, True), st + ["uq"], ["pa"], after=[("arr%d" % t, (t + 1) * before)] if t else [])
         V(ts(T.bits[:, 0:C], T.pa[:, 0:C], 0.0, pw, Alu.is_gt, Alu.mult), ["pa", "pw"], ["bits"])
         if t:
-            layer(0, True, False)
-            layer(1, True, False)
+            for b in range(3):
+                layer(b, True, True)
+                scaled(b)
         V(qz(T.bitq[:], T.bitss[:], T.bits[:]), ["bits", "bitpad"], ["bitq"])
-        P(mm(T.po[:, 0:128], *kside(0), T.bitq[:], T.bitss[:], True, True), ["kq0", "bitq"], ["po"])
-        P(mm(T.pc[:, 0:128], *kside(1), T.bitq[:], T.bitss[:], True, True), ["kq0", "bitq"], ["pc"])
-        V(ts(T.off[:], T.po[:, 0:64], bcol, None, Alu.add), ["po", "cf"], ["off"])
-        if t:
-            layer(2, True, False)
-            layer(3, True, False)
-        else:
-            V(qz(T.eq[:], T.es[:], T.et[:]), ["e0", "e1", "e2", "e3"], ["eq"])
-        gather("v", T.bt[:, 0:512], win, T.off[:, 0:32], wkey + ["off"], "bta")
-        gather("s", T.bt[:, 512:1024], win, T.off[:, 32:64], wkey + ["off"], "btb")
-        S(act(T.own[:], T.po[:, 0:64]), ["po"], ["own"])
-        V(qz(T.bq[:], T.bs[:], T.bt[:]), ["bta", "btb"], ["bq"])
+        for j in ((1, 0) if t else (0, 1)):
+            P(mm((T.po, T.pc)[j][:, 0:128], *kside(j), T.bitq[:], T.bitss[:], True, True), ["kq0", "bitq"], [("po", "pc")[j]])
         if t == 0:
+            V(ts(T.off[:], T.po[:, 0:64], bcol, None, Alu.add), ["po", "cf"], ["off"])
+            V(qz(T.eq[:], T.es[:], T.et[:]), ["e0", "e1", "e2", "e3"], ["eq"])
+            gather("v", T.bt[:, 0:512], T.pool[:, 0:lo], T.off[:, 0:32], ["pool_m", "off"], "bta")
+            gather("s", T.bt[:, 512:1024], T.pool[:, 0:lo], T.off[:, 32:64], ["pool_m", "off"], "btb")
+            S(act(T.own[:], T.po[:, 0:64]), ["po"], ["own"])
+            V(qz(T.bq[:], T.bs[:], T.bt[:]), ["bta", "btb"], ["bq"])
             layer(0, True, False)
             layer(1, True, False)
-        for b in range(4):
-            unpack(b, T.bq[:], T.bs[:], "bq", t == 0 and b > 1, t != 0 or b < 2)
-        if t == 0:
+            for b in range(4):
+                unpack(b, T.bq[:], T.bs[:], ["bq"], b > 1, b < 2)
             layer(2, False, True)
             layer(3, False, True)
-        for j in range(EARLY):
-            compare(j)
-        for b in range(4):
-            if b % 2 == 0:
-                S(act(T.yt[:, b:4 * C:4], banks[b][:, 0:C], 0.015625), ["pr%d" % b], ["yt%d" % b])
-            else:
-                V(ts(T.yt[:, b:4 * C:4], banks[b][:, 0:C], 0.015625, None, Alu.mult), ["pr%d" % b], ["yt%d" % b])
-        V(qz(yc[:], ys[:], T.yt[:]), ["yt%d" % b for b in range(4)], ["yq%d" % t])
-        dst = T.cores[(rank - VISITS + 1) % n] if final else T.cores[(rank + 1) % n]
-        hop(T["l%dc" % (t + 1)][:].bitcast(dt.uint8), yc[:].bitcast(dt.uint8), "arr3c" if final else "arr%d" % (t + 1), dst, "yq%d" % t)
-        hop(T.fins[:, 0:C] if final else T["l%ds" % (t + 1)][:], ys[:], "arr%d" % (t + 1), dst, "yq%d" % t)
-        P(mm(T.ps[:, 0:128], *kside(1), T.bitq[:], T.bitss[:], True, False), ["kq0", "bitq"], ["ps"])
-        for b in range(3):
-            written(b)
-        for j in range(EARLY, SHIFTS):
-            compare(j)
-        V(qz(T.flq[:], T.fls[:], T.fl[:]), ["fl%d" % j for j in range(SHIFTS)], ["flq"])
-        if t == 0:
-            written(3)
+            V(qz(T.mq[:], T.mqs[:], T.pool[:, 0:4 * M]), ["pool_m"], ["mq"])
+            for b in range(4):
+                if b % 2 == 0:
+                    S(act(T.yt[:, b:4 * C:4], banks[b][:, 0:C], 0.015625), ["pr%d" % b], ["yt%d" % b])
+                else:
+                    V(ts(T.yt[:, b:4 * C:4], banks[b][:, 0:C], 0.015625, None, Alu.mult), ["pr%d" % b], ["yt%d" % b])
+            V(qz(yc[:], ys[:], T.yt[:]), ["yt%d" % b for b in range(4)] + ["yta", "ytb"], yq)
+            hop(land[:].bitcast(dt.uint8), yc[:].bitcast(dt.uint8), csem, dst, yq[1])
+            hop(T.l1s[:], ys[:], "arr1", dst, yq[1])
+            first_map(0)
+            first_map(1)
+            for b in range(4):
+                written(b)
+            for j in range(SHIFTS):
+                compare(j)
+            pack_flags()
             late_constants()
-        P(mm(T.ps[:, 0:128], *kside(2), T.flq[:, 0:128], T.fls[:, 0:128], False, False), ["kq1", "flq"], ["ps"])
-        P(mm(T.ps[:, 0:128], *kside(3), T.flq[:, 64:192], T.fls[:, 64:192], False, True), ["kq1", "flq"], ["ps"])
-        if t:
-            written(3)
+            first_map(2)
+            first_map(3)
+            flags()
+            pack_written()
+        else:
+            layer(3, True, True)
+            V(lambda: v.tensor_tensor_scan(T.v1[:], T.kscan[:, 0:64], T.pc[:, 0:64], 0.0, Alu.mult, Alu.add), ["kscan", "pc"], ["v1"])
+            V(ts(T.r16[:], T.v1[:, 3:64:4], scol4, None, Alu.mult), ["v1", "scol4"], ["r16"])
+            S(act(T.own[:], T.po[:, 0:64]), ["po"], ["own"])
+            gather("s", T.look[:], T.tab[:, 0:M], T.r16[:], ["tab", "r16"], "look")
+            scaled(3)
+            for j in range(SHIFTS):
+                compare(j)
+            V(lambda: v.tensor_tensor_scan(T.scan[:, 0:C], T.kscan[:, 0:C], T.look[:], 0.0, Alu.mult, Alu.add), ["kscan", "look"], ["scana"])
+            V(ts(T.off[:], T.scan[:, 3:C:4], scol, bcol, Alu.mult, Alu.add), ["scana", "scol", "cf"], ["off"])
+            dk = ["dpm%d" % b for b in range(4)] + ["dp%d_%d" % (a, b) for a in range(t) for b in range(4)]
+            for h in range(2):
+                V(lambda h=h, lo=lo: v.tensor_tensor(T.yt[:, 4 * H * h:4 * H * h + 4 * H], T.dpool[:, 0:lo].indirect(T.off[:, 32 * h:32 * h + 32]),
+                                                     T.rt[:, 4 * H * h:4 * H * h + 4 * H], Alu.add),
+                  dk + ["off"] + ["rt%d" % b for b in range(4)], ["yt" + "ab"[h]])
+                V(qz(yc[:, H * h:H * h + H], ys[:, H * h:H * h + H], T.yt[:, 4 * H * h:4 * H * h + 4 * H]), ["yt" + "ab"[h]], [yq[h]])
+                hop(land[:, H * h:H * h + H].bitcast(dt.uint8), yc[:, H * h:H * h + H].bitcast(dt.uint8), csem, dst, yq[h])
+                if h == 0:
+                    pack_flags()
+                    flags()
+            hop(T.fins[:, 0:C] if final else T["l%ds" % (t + 1)][:], ys[:], "arr%d" % (t + 1), dst, yq[1])
+            for b in range(4):
+                written(b)
         V(lambda: v.tensor_tensor_scan(T.v2[:], T.kscan[:, 0:64], T.ps[:, 0:64], 0.0, Alu.mult, Alu.add), ["kscan", "ps"], ["v2"])
         for h in range(2):
             V(ts(T.o16[:, h:16:2], T.v2[:, 3 + 4 * h:64:8], scol4, T.spare[:, h:h + 1], Alu.mult, Alu.min), ["v2", "scol4", "spare"], ["o16%d" % h])
         for k in range(7, -1, -1):
             V(lambda k=k, t=t: v.tensor_copy(T.tab[:].indirect(T.o16[:, 2 * k:2 * k + 2]), T.val[:, C * t + 32 * k:C * t + 32 * k + 32]),
               ["o160", "o161", "val0", "val1"], ["tab"])
-        pk = ["pool_m"] + ["pool%d_%d" % (a, b) for a in range(t + 1) for b in range(4)]
-        mc, pwin = T["mc%d" % (t + 1)], T.pool[:, 0:lo + 4 * C]
+            if k == 3 and t == 1:
+                pack_written()
         if not final:
-            map_offsets(0, SPLIT, "a")
-            map_offsets(SPLIT, 128, "b")
-            gather("s", mc[:, 0:16 * SPLIT], pwin, T.moff[:, 0:SPLIT], pk + ["moffa"], "mc%da" % (t + 1))
-            gather("v", mc[:, 16 * SPLIT:4 * M], pwin, T.moff[:, SPLIT:128], pk + ["moffb"], "mc%db" % (t + 1))
+            for b in range(4):
+                rewritten(b)
         else:
+            pk = ["pool_m"] + ["pool%d_%d" % (a, b) for a in range(t + 1) for b in range(4)]
+            mc, pwin = T.mc, T.pool[:, 0:lo + 4 * C]
             map_offsets(0, 64, "a")
             map_offsets(64, 128, "b")
             for a, key in ((0, "a"), (64, "b")):
@@ -291,7 +334,7 @@ def rank_program(g, core, T, topo):
                 gather("v", mc[:, 16 * (a + LAST):16 * (a + 64)], pwin, T.moff[:, a + LAST:a + 64], pk + ["moff" + key], "mv" + key)
                 V(qz(T.qmc[:, 4 * a:4 * a + C], T.fins[:, C + 4 * a:2 * C + 4 * a], mc[:, 16 * a:16 * a + 4 * C]), ["ms" + key, "mv" + key], ["qm" + key])
 
-    codes, both = [("arr3c", home)], [("arr3c", home), ("arr3", home)]
+    codes, both = [("arr3c", 2 * home)], [("arr3c", 2 * home), ("arr3", home)]
     P(mm(T.pa[:, 0:C], *wside(0), T.l3c[:], T.fins[:, 0:C], True, True), ["w0", "ws"], ["pa"], after=both)
     load("y", T.oc[:, 4 * C:8 * C], T.qmc[:, 0:C].bitcast(dt.uint8), ["qma"], (), "dma")
     load("y", T.oc[:, 0:4 * C], T.l3c[:].bitcast(dt.uint8), (), (), "dsc", after=codes)

@@ -4,7 +4,10 @@ C, M, VISITS = 256, 512, 3
 X4, U8, BF, F32, U16, I32 = "float8_e4m3fn_x4", "uint8", "bfloat16", "float32", "uint16", "int32"
 BIG, BASE = 16384.0, 4194304.0
 SHIFTS = 8
-LAST = 40
+GV = (20, 28, 28)
+LAST = 36
+H = C // 2
+EW = 516
 
 
 def _sb(n, d):
@@ -14,27 +17,26 @@ def _sb(n, d):
 SCRATCH = {
     "xt": _sb(4 * C, BF), "ut": _sb(512, BF), "pool": _sb(4 * M + VISITS * 4 * C, BF),
     "wq": _sb(512, X4), "wsq": _sb(512, U8), "uq": _sb(128, X4), "usq": _sb(128, U8),
-    "l0c": _sb(C, X4), "l0s": _sb(C, U8), "l1c": _sb(C, X4), "l1s": _sb(C, U8), "l2c": _sb(C, X4), "l2s": _sb(C, U8),
+    "aq": _sb(192 + C, X4), "aqs": _sb(192 + C, U8), "wk": _sb(768, BF),
+    "l1c": _sb(C, X4), "l1s": _sb(C, U8), "l2c": _sb(C, X4), "l2s": _sb(C, U8),
     "l3c": _sb(C, X4), "fins": _sb(C + M, U8), "qmc": _sb(M, X4),
     "y0c": _sb(C, X4), "y0s": _sb(C, U8), "y1c": _sb(C, X4), "y1s": _sb(C, U8), "y2c": _sb(C, X4), "y2s": _sb(C, U8),
-    "bits": _sb(512, BF), "bitq": _sb(128, X4), "bitss": _sb(128, U8),
-    "off": _sb(64, U16), "own": _sb(64, F32), "bt": _sb(4 * C, BF), "bq": _sb(C, X4), "bs": _sb(C, U8), "yt": _sb(4 * C, BF),
-    "fl": _sb(768, BF), "flq": _sb(192, X4), "fls": _sb(192, U8),
-    "v2": _sb(64, F32), "o16": _sb(16, U16),
+    "off": _sb(64, U16), "own": _sb(64, F32), "own0": _sb(64, F32), "bt": _sb(4 * C, BF), "bq": _sb(C, X4), "bs": _sb(C, U8), "yt": _sb(4 * C, BF),
+    "v1": _sb(64, F32), "v2": _sb(64, F32),
+    "rs1": _sb(16, U16), "rs2": _sb(16, U16), "ra1": _sb(16, U16), "ra2": _sb(16, U16),
+    "oa0": _sb(16, U16), "os1": _sb(16, U16), "os2": _sb(16, U16), "oa1": _sb(16, U16), "oa2": _sb(16, U16),
     "tab": _sb(M + 256, F32), "val": _sb(VISITS * C, F32), "scan": _sb(M, F32), "moff": _sb(128, U16),
-    "mc": _sb(4 * M, BF), "v1": _sb(64, F32), "r16": _sb(16, U16), "look": _sb(C, F32),
-    "dpool": _sb(4 * M + (VISITS - 1) * 4 * C, BF), "rt": _sb(4 * C, F32),
-    "mq": _sb(M, X4), "mqs": _sb(M, U8), "nq": _sb(C, X4), "nqs": _sb(C, U8),
-    "zero": _sb(1024, BF), "c64": _sb(128, BF), "ident": _sb(128, BF), "et": _sb(2048, BF), "eq": _sb(512, X4), "es": _sb(512, U8),
-    "kt": _sb(2048, BF), "kq": _sb(512, X4), "ks": _sb(512, U8),
+    "mc": _sb(4 * M, BF), "look": _sb(C, F32), "seq": _sb(C, F32),
+    "c64": _sb(EW, BF), "ident": _sb(128, BF), "et": _sb(2 * EW, BF), "eq": _sb(512, X4), "es": _sb(512, U8),
+    "kt": _sb(1536, BF), "kq": _sb(384, X4), "ks": _sb(384, U8),
     "iq": _sb(1, I32), "ci": _sb(8, I32), "cf": _sb(8, F32), "col": _sb(8, F32), "i18": _sb(18, F32), "t18": _sb(18, F32),
-    "ia": _sb(128, BF), "ic": _sb(128, BF), "i4": _sb(M, BF), "t4": _sb(4, F32),
-    "spare": _sb(2, F32), "kscan": _sb(M, BF), "ysb": _sb(C, F32),
+    "ia": _sb(128, BF), "ic": _sb(128, BF), "i4": _sb(C, BF), "t4": _sb(4, F32),
+    "spare": _sb(2, F32), "kscan": _sb(C, BF), "ysb": _sb(C, F32),
     "pa": ("psum", [128, 512], F32), "po": ("psum", [128, 512], F32), "pc": ("psum", [128, 512], F32), "ps": ("psum", [128, 512], F32),
     "pr0": ("psum", [128, 512], F32), "pr1": ("psum", [128, 512], F32), "pr2": ("psum", [128, 512], F32), "pr3": ("psum", [128, 512], F32),
 }
 DMAS = ["dx", "du", "dm", "dws", "dwa", "dwb", "dy", "dsc", "dma", "dmb", "ds0", "ds1", "ds2", "ds3"]
-SEMAPHORES = ["qv", "qs", "qt", "qg", "arr1", "arr2", "arr3", "arr3c", "sent"] + DMAS
+SEMAPHORES = ["qv", "qs", "qt", "qg", "arr1", "arr2", "arr3", "arr3c", "ar1", "ar2", "ao1", "ao2", "sent"] + DMAS
 PSUM = ("pa", "po", "pc", "ps", "pr0", "pr1", "pr2", "pr3")
 
 
@@ -97,12 +99,17 @@ def rank_program(g, core, T, topo):
     def qz(c, sc, t):
         return lambda: v.quantize_mx(c, sc, t)
 
+    def scan(out, data, width):
+        return lambda: v.tensor_tensor_scan(out, T.kscan[:, 0:width], data, 0.0, Alu.mult, Alu.add)
+
     def iota(out, pattern, base, cm, small=True):
         if small:
             return lambda: g.iota(out, pattern, base, cm, allow_small_or_imprecise_dtypes=True)
         return lambda: g.iota(out, pattern, base, cm)
 
-    def act(out, in_, scale=None):
+    def act(out, in_, scale=None, bias=None):
+        if bias is not None:
+            return lambda: s.activation(out, in_, Act.Identity, bias=bias)
         if scale is None:
             return lambda: s.activation(out, in_, Act.Copy)
         return lambda: s.activation(out, in_, Act.Copy, scale=scale)
@@ -117,54 +124,64 @@ def rank_program(g, core, T, topo):
     load("y", T.wq[:, 0:256].bitcast(dt.uint8), T.wc[:, 0:1024], (), ["w0", "w1"], "dwa")
     load("y", T.wq[:, 256:512].bitcast(dt.uint8), T.wc[:, 1024:2048], (), ["w2", "w3"], "dwb")
 
+    fls = ["fl%d" % j for j in range(SHIFTS)]
     G(iota(T.iq[:], [[0, 1]], 0, 1, False), (), ["iq"])
-    G(iota(T.i18[:], [[1, 18]], -2, 0), (), ["i18"])
     G(iota(T.ia[:], [[4, 8], [1, 4], [0, 4]], 0, 0), (), ["ia"])
+    G(iota(T.i18[:], [[1, 18]], -2, 0), (), ["i18"])
     G(iota(T.ic[:], [[4, 8], [0, 4], [1, 4]], 0, 0), (), ["ic"])
     V(lambda: v.memset(T.c64[:], 64.0), (), ["c64"])
-    V(lambda: v.memset(T.zero[:], 0.0), (), ["zero"])
-    G(lambda: g.affine_select(T.ident[:], T.c64[:], [[-1, 128]], Alu.is_equal, 0.0, 0, 1), ["c64"], ["ident"])
-    G(iota(T.tab[:, 0:M], [[4, M]], 0, 0), (), ["tab"])
-    G(iota(T.i4[:], [[0, M // 4], [1, 4]], 0, 0), (), ["i4"])
+    G(lambda: g.affine_select(T.ident[:], T.c64[:, 0:128], [[-1, 128]], Alu.is_equal, 0.0, 0, 1), ["c64"], ["ident"])
+    G(iota(T.i4[:], [[0, C // 4], [1, 4]], 0, 0), (), ["i4"])
+    G(iota(T.seq[:], [[4, C]], 0, 0), (), ["seq"])
     G(iota(T.spare[:], [[128, 2]], M, 1), (), ["spare"])
-    V(ts(T.ci[:, 0:1], T.iq[:], 2, None, Alu.logical_shift_right), ["iq"], ["ci0"])
+    for h in range(2):
+        S(act(T.et[:, EW * h:EW * h + EW], T.c64[:], 0.0), ["c64"], ["et%d" % h])
+    S(act(T.wk[:, C:768], T.c64[:, 0:512], 0.0), ["c64"], fls)
+    for h in range(2):
+        S(act(T.et[:, EW * h + 2 + h:EW * h + 512 + h:4], T.ident[:]), ["ident"], ["et%d" % h])
     V(ts(T.ci[:, 1:2], T.iq[:], 2, 28, Alu.logical_shift_right, Alu.bitwise_and), ["iq"], ["ci1"])
+    V(ts(T.ci[:, 4:5], T.iq[:], 15, None, Alu.bitwise_and), ["iq"], ["ci4"])
+    V(ts(T.ci[:, 0:1], T.iq[:], 2, None, Alu.logical_shift_right), ["iq"], ["ci0"])
     V(ts(T.ci[:, 2:3], T.iq[:], 2, 3, Alu.logical_shift_right, Alu.bitwise_and), ["iq"], ["ci2"])
     V(ts(T.ci[:, 3:4], T.iq[:], 3, None, Alu.bitwise_and), ["iq"], ["ci3"])
-    V(ts(T.ci[:, 4:5], T.iq[:], 15, None, Alu.bitwise_and), ["iq"], ["ci4"])
-    V(lambda: v.memset(T.bits[:, C:512], 0.0), (), ["bitpad"])
     V(lambda: v.tensor_copy(T.cf[:, 0:5], T.ci[:, 0:5]), ["ci0", "ci1", "ci2", "ci3", "ci4"], ["cf"])
     q4, g4, tau, bcol, icol = [T.cf[:, j:j + 1] for j in range(5)]
-    p2, pw, lt, scol, scol4 = [T.col[:, j:j + 1] for j in range(5)]
-    V(ts(T.t18[:], T.i18[:], icol, 1.0, Alu.is_lt, Alu.add), ["i18", "cf"], ["t18"])
+    p2, pw, ge, scol, scol4 = [T.col[:, j:j + 1] for j in range(5)]
     for t in range(4):
         V(ts(T.kt[:, t:512:4], T.ia[:], float(t), g4, Alu.subtract, Alu.is_equal), ["ia", "cf"], ["ka%d" % t])
+    V(ts(T.t18[:], T.i18[:], icol, 1.0, Alu.is_lt, Alu.add), ["i18", "cf"], ["t18"])
+    V(qz(T.kq[:, 0:128], T.ks[:, 0:128], T.kt[:, 0:512]), ["ka%d" % t for t in range(4)], ["kq0"])
     V(lambda: v.tensor_reduce(p2, T.t18[:], AxisListType.X, Alu.mult), ["t18"], ["p2"])
+    V(ts(T.kt[:, 1024:1536:4], T.ic[:], q4, BIG, Alu.is_equal, Alu.mult), ["ic", "cf"], ["kd0"])
+    V(ts(pw, icol, 9.0, p2, Alu.is_lt, Alu.mult), ["cf", "p2"], ["pw"])
+    V(qz(T.uq[:], T.usq[:], T.ut[:]), ["ut"], ["uq"])
     for t in range(4):
         V(ts(T.kt[:, 512 + t:1024:4], T.ic[:], float(t), g4, Alu.subtract, Alu.is_equal), ["ic", "cf"], ["kc%d" % t])
-    V(ts(pw, icol, 9.0, p2, Alu.is_lt, Alu.mult), ["cf", "p2"], ["pw"])
-    V(qz(T.kq[:, 0:256], T.ks[:, 0:256], T.kt[:, 0:1024]), ["ka%d" % t for t in range(4)] + ["kc%d" % t for t in range(4)], ["kq0"])
-    V(lambda: v.memset(T.fl[:], 0.0), (), ["fl%d" % j for j in range(SHIFTS)])
-    S(act(T.et[:, 0:1024], T.zero[:]), ["zero"], ["e0", "e1"])
-    S(act(T.et[:, 1024:2048], T.zero[:]), ["zero"], ["e2", "e3"])
-    for b in range(4):
-        S(act(T.et[:, 512 * b + b:512 * b + 512:4], T.ident[:]), ["ident"], ["e%d" % b])
-    S(lambda: s.activation(T.val[:, 0:M], T.tab[:, 0:M], Act.Identity, bias=float(4 * M)), ["tab"], ["val0"])
-    S(lambda: s.activation(T.val[:, M:M + C], T.tab[:, 0:C], Act.Identity, bias=float(8 * M)), ["tab"], ["val1"])
+    V(ts(ge, bcol, tau, BIG, Alu.is_ge, Alu.mult), ["cf"], ["ge"])
+    for t in range(1, 4):
+        S(act(T.kt[:, 1024 + t:1536:4], T.kt[:, 1024:1536:4]), ["kd0"], ["kd%d" % t])
+    S(act(T.tab[:, 0:C], T.seq[:]), ["seq"], ["tab"])
+    S(act(T.tab[:, C:M], T.seq[:], bias=float(4 * C)), ["seq"], ["tabb"])
 
-    def late_constants():
-        V(ts(lt, bcol, tau, BIG, Alu.is_lt, Alu.mult), ["cf"], ["lt"])
-        V(ts(T.t4[:], T.i4[:, 0:4], tau, 1.0 / BASE, Alu.is_le, Alu.max), ["i4", "cf"], ["t4"])
-        for t in range(1, 8):
-            V(ts(T.kt[:, 1024 + 512 * (t // 4) + t % 4:1536 + 512 * (t // 4):4], T.ic[:], q4, BIG, Alu.is_equal, Alu.mult), ["ic", "cf"], ["kd%d" % t])
-        V(ts(T.kt[:, 1024:1536:4], T.ic[:], q4, lt, Alu.is_equal, Alu.mult), ["ic", "cf", "lt"], ["kd0"])
-        V(lambda: v.tensor_reduce(scol, T.t4[:], AxisListType.X, Alu.mult), ["t4"], ["scol"])
-        V(qz(T.kq[:, 256:512], T.ks[:, 256:512], T.kt[:, 1024:2048]), ["kd%d" % t for t in range(8)], ["kq1"])
-        V(ts(T.kscan[:], T.i4[:], tau, BASE, Alu.is_gt, Alu.mult), ["i4", "cf"], ["kscan"])
-        V(ts(scol4, scol, 0.25, None, Alu.mult), ["scol"], ["scol4"])
+    def values(t):
+        S(act(T.val[:, C * t:C * t + C], T.seq[:], bias=float(4 * M + 4 * C * t)), ["seq"], ["val%d" % t])
 
-    V(qz(T.uq[:], T.usq[:], T.ut[:]), ["ut"], ["uq"])
-    V(qz(T.l0c[:], T.l0s[:], T.xt[:]), ["xt"], ["state0"])
+    def pack_e(b):
+        a = EW * (b % 2) + 2 - 2 * (b // 2)
+        V(qz(T.eq[:, 128 * b:128 * b + 128], T.es[:, 128 * b:128 * b + 128], T.et[:, a:a + 512]), ["et%d" % (b % 2)], ["eq%d" % b])
+
+    def pack_k():
+        V(qz(T.kq[:, 128:384], T.ks[:, 128:384], T.kt[:, 512:1536]), ["kc%d" % t for t in range(4)] + ["kd%d" % t for t in range(4)], ["kq1"])
+
+    def late_constants(i):
+        if i == 0:
+            V(ts(T.t4[:], T.i4[:, 0:4], tau, 1.0 / BASE, Alu.is_le, Alu.max), ["i4", "cf"], ["t4"])
+            V(ts(T.kscan[:], T.i4[:], tau, BASE, Alu.is_gt, Alu.mult), ["i4", "cf"], ["kscan"])
+            V(lambda: v.tensor_reduce(scol, T.t4[:], AxisListType.X, Alu.mult), ["t4"], ["scol"])
+        else:
+            V(ts(scol4, scol, 0.25, None, Alu.mult), ["scol"], ["scol4"])
+
+    V(qz(T.aq[:, 192:192 + C], T.aqs[:, 192:192 + C], T.xt[:]), ["xt"], ["state0"])
 
     banks = [T.pr0, T.pr1, T.pr2, T.pr3]
     engines = [0]
@@ -178,154 +195,191 @@ def rank_program(g, core, T, topo):
     def eside(b):
         return T.eq[:, 128 * b:128 * b + 128], T.es[:, 128 * b:128 * b + 128]
 
+    def work(a):
+        return T.aq[:, a:a + 128], T.aqs[:, a:a + 128]
+
     def map_offsets(a, z, key):
-        V(lambda: v.tensor_tensor_scan(T.scan[:, 4 * a:4 * z], T.kscan[:, 4 * a:4 * z], T.tab[:, 4 * a:4 * z], 0.0, Alu.mult, Alu.add),
-          ["kscan", "tab"], ["scan" + key])
+        V(scan(T.scan[:, 4 * a:4 * z], T.tab[:, 4 * a:4 * z], 4 * (z - a)), ["kscan", "tab", "tabb"], ["scan" + key])
         V(ts(T.moff[:, a:z], T.scan[:, 4 * a + 3:4 * z:4], scol, bcol, Alu.mult, Alu.add), ["scan" + key, "scol", "cf"], ["moff" + key])
 
-    def gather(q, out, win, offs, reads, key):
+    def gather(q, out, win, offs, reads, key, after=()):
         if q == "v":
-            V(lambda: v.tensor_copy(out, win.indirect(offs)), reads, [key])
+            V(lambda: v.tensor_copy(out, win.indirect(offs)), reads, [key], after=after)
         else:
-            S(lambda: s.activation(out, win.indirect(offs), Act.Copy), reads, [key])
+            S(lambda: s.activation(out, win.indirect(offs), Act.Copy), reads, [key], after=after)
 
-    def hop(out, in_, sem, dst, key):
+    def hop(out, in_, sem, dst, keys):
         rid, pid = topo.addr(dst, core)
         engines[0] += len(topo.engines(core, dst))
-        G(lambda: g.remote_dma(out, in_, T.sem[sem], T.sem.sent, pid, rid, topo.mask(core, dst)), [key], dma="remote")
+        G(lambda: g.remote_dma(out, in_, T.sem[sem], T.sem.sent, pid, rid, topo.mask(core, dst)), keys, dma="remote")
 
+    nxt = T.cores[(rank + 1) % n]
     before = len(topo.engines(T.cores[(rank - 1) % n], core))
     home = len(topo.engines(T.cores[(rank + VISITS - 1) % n], core))
 
-    H = C // 2
+    def product_a(c, sc, keys):
+        P(mm(T.pa[:, 0:C], T.uq[:], T.usq[:], c, sc, True, True), keys + ["uq"], ["pa"])
+
+    def bits():
+        V(ts(T.wk[:, 0:C], T.pa[:, 0:C], 0.0, pw, Alu.is_gt, Alu.mult), ["pa", "pw"], ["bits"])
+
+    def pack_bits():
+        V(qz(T.aq[:, 0:128], T.aqs[:, 0:128], T.wk[:, 0:512]), ["bits"] + fls[:4], ["bitq", "flq0"])
+
+    def sums(j):
+        P(mm((T.po, T.pc)[j][:, 0:128], *kside(j), *work(0), True, True), ["kq%d" % j, "bitq", "flq0"], [("po", "pc")[j]])
+
+    def owns():
+        S(act(T.own0[:], T.po[:, 0:64], bias=ge), ["po", "ge"], ["own0"])
+        S(act(T.own[:], T.po[:, 0:64]), ["po"], ["own"])
+
+    def compare(j):
+        a = C + 256 * (j // 4)
+        o = "own" if j else "own0"
+        V(lambda: v.tensor_tensor(T.wk[:, a + 4 * j + j % 4:a + 256:4], T.pc[:, 0:64 - j], T[o][:, j:64], Alu.is_equal), ["pc", o], ["fl%d" % j])
+
+    def pack_flags():
+        V(qz(T.aq[:, 64:192], T.aqs[:, 64:192], T.wk[:, C:768]), fls, ["flq0", "flq1"])
+
+    def flags():
+        P(mm(T.ps[:, 0:128], *kside(1), *work(0), True, False), ["kq1", "bitq", "flq0"], ["ps"])
+        P(mm(T.ps[:, 0:128], *kside(2), *work(64), False, False), ["kq1", "flq0", "flq1"], ["ps"])
+        P(mm(T.ps[:, 0:128], *kside(2), *work(128), False, True), ["kq1", "flq1", "state0"], ["ps"])
+
+    def slots_scan():
+        V(scan(T.v2[:], T.ps[:, 0:64], 64), ["kscan", "ps"], ["v2"])
+
+    def slots(t):
+        name = "os%d" % t if t else "oa0"
+        for h in range(2):
+            V(ts(T[name][:, h:16:2], T.v2[:, 3 + 4 * h:64:8], scol4, T.spare[:, h:h + 1], Alu.mult, Alu.min), ["v2", "scol4", "spare"], [name + "ab"[h]])
+        if t:
+            hop(T["oa%d" % t][:], T[name][:], "ao%d" % t, nxt, [name + "a", name + "b"])
+
+    def scatter(t, k):
+        V(lambda: v.tensor_copy(T.tab[:].indirect(T["oa%d" % t][:, 2 * k:2 * k + 2]), T.val[:, C * t + 32 * k:C * t + 32 * k + 32]),
+          ["oa0a", "oa0b", "val%d" % t], ["tab", "tabb"], after=[("ao%d" % t, before)] if t else [])
+
+    def unpack(b, c, sc, keys, start, stop):
+        P(mm(banks[b][:, 0:C], *eside(b), c, sc, start, stop), keys + ["eq%d" % b], ["pr%d" % b])
+
+    def scaled(q, out, b, key):
+        if q == "s":
+            S(act(out, banks[b][:, 0:C], 0.015625), ["pr%d" % b], [key])
+        else:
+            V(ts(out, banks[b][:, 0:C], 0.015625, None, Alu.mult), ["pr%d" % b], [key])
+
     for t in range(VISITS):
-        sc_, ss_ = T["l%dc" % t][:], T["l%ds" % t][:]
+        sc_, ss_ = (T["l%dc" % t][:], T["l%ds" % t][:]) if t else (T.aq[:, 192:192 + C], T.aqs[:, 192:192 + C])
         yc, ys = T["y%dc" % t], T["y%ds" % t]
         st = ["state0"] if t == 0 else []
         final = t + 1 == VISITS
         lo = 4 * M + 4 * C * t
-        yq = ["yqa%d" % t, "yqb%d" % t]
-        dst = T.cores[(rank - VISITS + 1) % n] if final else T.cores[(rank + 1) % n]
-        land, csem = T["l%dc" % (t + 1)], "arr3c" if final else "arr%d" % (t + 1)
+        yq = ["yq%d" % t]
+        pk = ["pool_m"] + ["pool%d_%d" % (a, b) for a in range(t) for b in range(4)]
+        gv = 16 * GV[t]
 
         def layer(b, start, stop):
-            P(mm(banks[b][:, 0:C], *wside(b), sc_, ss_, start, stop), st + ["w%d" % b, "ws"], ["pr%d" % b])
+            P(mm(banks[b][:, 0:C], *wside(b), sc_, ss_, start, stop), st + ["w%d" % b, "ws"], ["pr%d" % b], after=[("arr%d" % t, 2 * before)] if t else [])
 
-        def unpack(b, c, sc2, keys, start, stop):
-            P(mm(banks[b][:, 0:C], *eside(b), c, sc2, start, stop), keys + ["eq"], ["pr%d" % b])
-
-        def compare(j):
-            h = j // 4
-            V(lambda: v.tensor_tensor(T.fl[:, 256 * h + 4 * j + j % 4:256 * h + 256:4], T.pc[:, 0:64 - j], T.own[:, j:64], Alu.is_equal),
-              ["pc", "own"], ["fl%d" % j])
-
-        def pack_flags():
-            V(qz(T.flq[:], T.fls[:], T.fl[:]), ["fl%d" % j for j in range(SHIFTS)], ["flq"])
-
-        def flags():
-            P(mm(T.ps[:, 0:128], *kside(1), T.bitq[:], T.bitss[:], True, False), ["kq0", "bitq"], ["ps"])
-            P(mm(T.ps[:, 0:128], *kside(2), T.flq[:, 0:128], T.fls[:, 0:128], False, False), ["kq1", "flq"], ["ps"])
-            P(mm(T.ps[:, 0:128], *kside(3), T.flq[:, 64:192], T.fls[:, 64:192], False, True), ["kq1", "flq"], ["ps"])
-
-        def written(b):
+        def written(b, q="s"):
             unpack(b, yc[:], ys[:], yq, True, True)
-            S(act(T.pool[:, lo + b:lo + 4 * C:4], banks[b][:, 0:C], 0.015625), ["pr%d" % b], ["pool%d_%d" % (t, b)])
+            scaled(q, T.pool[:, lo + b:lo + 4 * C:4], b, "pool%d_%d" % (t, b))
 
-        def pack_written():
-            V(qz(T.nq[:], T.nqs[:], T.pool[:, lo:lo + 4 * C]), ["pool%d_%d" % (t, b) for b in range(4)], ["nq"])
+        def read_b():
+            gather("s", T.bt[:, gv:4 * C], T.pool[:, 0:lo], T.off[:, GV[t]:64], pk + ["off"], "btb")
+            gather("v", T.bt[:, 0:gv], T.pool[:, 0:lo], T.off[:, 0:GV[t]], pk + ["off"], "bta")
 
-        def rewritten(b):
-            unpack(b, T.nq[:], T.nqs[:], ["nq"], True, True)
-            S(act(T.dpool[:, lo + b:lo + 4 * C:4], banks[b][:, 0:C], 0.015625), ["pr%d" % b], ["dp%d_%d" % (t, b)])
-
-        def first_map(b):
-            name = ("pa", "po")[b % 2]
-            P(mm(T[name][:], *eside(b), T.mq[:], T.mqs[:], True, True), ["mq", "eq"], [name])
-            S(act(T.dpool[:, b:4 * M:4], T[name][:], 0.015625), [name], ["dpm%d" % b])
-
-        def scaled(b):
-            S(act(T.rt[:, b:4 * C:4], banks[b][:, 0:C], 0.015625), ["pr%d" % b], ["rt%d" % b])
-
-        P(mm(T.pa[:, 0:C], T.uq[:], T.usq[:], sc_, ss_, True, True), st + ["uq"], ["pa"], after=[("arr%d" % t, (t + 1) * before)] if t else [])
-        V(ts(T.bits[:, 0:C], T.pa[:, 0:C], 0.0, pw, Alu.is_gt, Alu.mult), ["pa", "pw"], ["bits"])
-        if t:
-            for b in range(3):
-                layer(b, True, True)
-                scaled(b)
-        V(qz(T.bitq[:], T.bitss[:], T.bits[:]), ["bits", "bitpad"], ["bitq"])
-        for j in ((1, 0) if t else (0, 1)):
-            P(mm((T.po, T.pc)[j][:, 0:128], *kside(j), T.bitq[:], T.bitss[:], True, True), ["kq0", "bitq"], [("po", "pc")[j]])
-        if t == 0:
-            V(ts(T.off[:], T.po[:, 0:64], bcol, None, Alu.add), ["po", "cf"], ["off"])
-            V(qz(T.eq[:], T.es[:], T.et[:]), ["e0", "e1", "e2", "e3"], ["eq"])
-            gather("v", T.bt[:, 0:512], T.pool[:, 0:lo], T.off[:, 0:32], ["pool_m", "off"], "bta")
-            gather("s", T.bt[:, 512:1024], T.pool[:, 0:lo], T.off[:, 32:64], ["pool_m", "off"], "btb")
-            S(act(T.own[:], T.po[:, 0:64]), ["po"], ["own"])
+        def pack_b():
             V(qz(T.bq[:], T.bs[:], T.bt[:]), ["bta", "btb"], ["bq"])
+
+        if t == 0:
+            product_a(sc_, ss_, st)
+            pack_k()
+            bits()
+            pack_bits()
+            sums(0)
+            sums(1)
+            pack_e(0)
+            V(ts(T.off[:], T.po[:, 0:64], bcol, None, Alu.add), ["po", "cf"], ["off"])
+            pack_e(2)
+            read_b()
+            owns()
+            values(0)
+            pack_e(1)
+            pack_e(3)
+            late_constants(0)
+            pack_b()
             layer(0, True, False)
             layer(1, True, False)
             for b in range(4):
                 unpack(b, T.bq[:], T.bs[:], ["bq"], b > 1, b < 2)
             layer(2, False, True)
             layer(3, False, True)
-            V(qz(T.mq[:], T.mqs[:], T.pool[:, 0:4 * M]), ["pool_m"], ["mq"])
+            late_constants(1)
+            for j in range(4):
+                compare(j)
+        else:
+            lists = [("ar%d" % t, before)]
+            gather("s", T.look[:, H:C], T.tab[:, 0:M], T["ra%d" % t][:, 8:16], ["tab", "tabb"], "lookb", after=lists)
+            gather("v", T.look[:, 0:H], T.tab[:, 0:M], T["ra%d" % t][:, 0:8], ["tab", "tabb"], "looka", after=lists)
             for b in range(4):
-                if b % 2 == 0:
-                    S(act(T.yt[:, b:4 * C:4], banks[b][:, 0:C], 0.015625), ["pr%d" % b], ["yt%d" % b])
-                else:
-                    V(ts(T.yt[:, b:4 * C:4], banks[b][:, 0:C], 0.015625, None, Alu.mult), ["pr%d" % b], ["yt%d" % b])
-            V(qz(yc[:], ys[:], T.yt[:]), ["yt%d" % b for b in range(4)] + ["yta", "ytb"], yq)
-            hop(land[:].bitcast(dt.uint8), yc[:].bitcast(dt.uint8), csem, dst, yq[1])
-            hop(T.l1s[:], ys[:], "arr1", dst, yq[1])
-            first_map(0)
-            first_map(1)
+                layer(b, True, False)
+            V(scan(T.scan[:, 0:C], T.look[:], C), ["kscan", "looka", "lookb"], ["scana"])
+            slots_scan()
+            V(ts(T.off[:], T.scan[:, 3:C:4], scol, bcol, Alu.mult, Alu.add), ["scana", "scol", "cf"], ["off"])
+            read_b()
+            slots(t)
+            pack_b()
             for b in range(4):
+                unpack(b, T.bq[:], T.bs[:], ["bq"], False, True)
+        for b in range(4):
+            scaled("sv"[b % 2], T.yt[:, b:4 * C:4], b, "yt%d" % b)
+            if t == 0 and b == 1:
+                for j in range(4, 8):
+                    compare(j)
+                pack_flags()
+                flags()
+        V(qz(yc[:], ys[:], T.yt[:]), ["yt%d" % b for b in range(4)], yq)
+        if not final:
+            hop(T["l%dc" % (t + 1)][:].bitcast(dt.uint8), yc[:].bitcast(dt.uint8), "arr%d" % (t + 1), nxt, yq)
+            product_a(yc[:], ys[:], yq)
+            if t == 0:
+                slots_scan()
+                slots(0)
+            else:
+                scatter(t, 7)
+            bits()
+            written(0)
+            pack_bits()
+            sums(1)
+            sums(0)
+            scatter(t, 6 if t else 7)
+            name = "rs%d" % (t + 1)
+            V(scan(T.v1[:], T.pc[:, 0:64], 64), ["kscan", "pc"], ["v1"])
+            V(ts(T[name][:], T.v1[:, 3:64:4], scol4, None, Alu.mult), ["v1", "scol4"], [name])
+            hop(T["ra%d" % (t + 1)][:], T[name][:], "ar%d" % (t + 1), nxt, [name])
+            hop(T["l%ds" % (t + 1)][:], ys[:], "arr%d" % (t + 1), nxt, yq)
+            owns()
+            for b in range(1, 4):
                 written(b)
+            values(t + 1)
             for j in range(SHIFTS):
+                k = (5 if t else 6) - j
+                if k >= 0:
+                    scatter(t, k)
                 compare(j)
             pack_flags()
-            late_constants()
-            first_map(2)
-            first_map(3)
             flags()
-            pack_written()
         else:
-            layer(3, True, True)
-            V(lambda: v.tensor_tensor_scan(T.v1[:], T.kscan[:, 0:64], T.pc[:, 0:64], 0.0, Alu.mult, Alu.add), ["kscan", "pc"], ["v1"])
-            V(ts(T.r16[:], T.v1[:, 3:64:4], scol4, None, Alu.mult), ["v1", "scol4"], ["r16"])
-            S(act(T.own[:], T.po[:, 0:64]), ["po"], ["own"])
-            gather("s", T.look[:], T.tab[:, 0:M], T.r16[:], ["tab", "r16"], "look")
-            scaled(3)
-            for j in range(SHIFTS):
-                compare(j)
-            V(lambda: v.tensor_tensor_scan(T.scan[:, 0:C], T.kscan[:, 0:C], T.look[:], 0.0, Alu.mult, Alu.add), ["kscan", "look"], ["scana"])
-            V(ts(T.off[:], T.scan[:, 3:C:4], scol, bcol, Alu.mult, Alu.add), ["scana", "scol", "cf"], ["off"])
-            dk = ["dpm%d" % b for b in range(4)] + ["dp%d_%d" % (a, b) for a in range(t) for b in range(4)]
-            for h in range(2):
-                V(lambda h=h, lo=lo: v.tensor_tensor(T.yt[:, 4 * H * h:4 * H * h + 4 * H], T.dpool[:, 0:lo].indirect(T.off[:, 32 * h:32 * h + 32]),
-                                                     T.rt[:, 4 * H * h:4 * H * h + 4 * H], Alu.add),
-                  dk + ["off"] + ["rt%d" % b for b in range(4)], ["yt" + "ab"[h]])
-                V(qz(yc[:, H * h:H * h + H], ys[:, H * h:H * h + H], T.yt[:, 4 * H * h:4 * H * h + 4 * H]), ["yt" + "ab"[h]], [yq[h]])
-                hop(land[:, H * h:H * h + H].bitcast(dt.uint8), yc[:, H * h:H * h + H].bitcast(dt.uint8), csem, dst, yq[h])
-                if h == 0:
-                    pack_flags()
-                    flags()
-            hop(T.fins[:, 0:C] if final else T["l%ds" % (t + 1)][:], ys[:], "arr%d" % (t + 1), dst, yq[1])
+            dst = T.cores[(rank - VISITS + 1) % n]
+            hop(T.l3c[:].bitcast(dt.uint8), yc[:].bitcast(dt.uint8), "arr3c", dst, yq)
+            hop(T.fins[:, 0:C], ys[:], "arr3", dst, yq)
             for b in range(4):
                 written(b)
-        V(lambda: v.tensor_tensor_scan(T.v2[:], T.kscan[:, 0:64], T.ps[:, 0:64], 0.0, Alu.mult, Alu.add), ["kscan", "ps"], ["v2"])
-        for h in range(2):
-            V(ts(T.o16[:, h:16:2], T.v2[:, 3 + 4 * h:64:8], scol4, T.spare[:, h:h + 1], Alu.mult, Alu.min), ["v2", "scol4", "spare"], ["o16%d" % h])
-        for k in range(7, -1, -1):
-            V(lambda k=k, t=t: v.tensor_copy(T.tab[:].indirect(T.o16[:, 2 * k:2 * k + 2]), T.val[:, C * t + 32 * k:C * t + 32 * k + 32]),
-              ["o160", "o161", "val0", "val1"], ["tab"])
-            if k == 3 and t == 1:
-                pack_written()
-        if not final:
-            for b in range(4):
-                rewritten(b)
-        else:
-            pk = ["pool_m"] + ["pool%d_%d" % (a, b) for a in range(t + 1) for b in range(4)]
+            for k in range(7, -1, -1):
+                scatter(t, k)
+            pk = pk + ["pool%d_%d" % (t, b) for b in range(4)]
             mc, pwin = T.mc, T.pool[:, 0:lo + 4 * C]
             map_offsets(0, 64, "a")
             map_offsets(64, 128, "b")
@@ -334,10 +388,10 @@ def rank_program(g, core, T, topo):
                 gather("v", mc[:, 16 * (a + LAST):16 * (a + 64)], pwin, T.moff[:, a + LAST:a + 64], pk + ["moff" + key], "mv" + key)
                 V(qz(T.qmc[:, 4 * a:4 * a + C], T.fins[:, C + 4 * a:2 * C + 4 * a], mc[:, 16 * a:16 * a + 4 * C]), ["ms" + key, "mv" + key], ["qm" + key])
 
-    codes, both = [("arr3c", 2 * home)], [("arr3c", 2 * home), ("arr3", home)]
+    codes, both = [("arr3c", home)], [("arr3c", home), ("arr3", home)]
     P(mm(T.pa[:, 0:C], *wside(0), T.l3c[:], T.fins[:, 0:C], True, True), ["w0", "ws"], ["pa"], after=both)
-    load("y", T.oc[:, 4 * C:8 * C], T.qmc[:, 0:C].bitcast(dt.uint8), ["qma"], (), "dma")
     load("y", T.oc[:, 0:4 * C], T.l3c[:].bitcast(dt.uint8), (), (), "dsc", after=codes)
+    load("y", T.oc[:, 4 * C:8 * C], T.qmc[:, 0:C].bitcast(dt.uint8), ["qma"], (), "dma")
     load("y", T.oc[:, 8 * C:12 * C], T.qmc[:, C:2 * C].bitcast(dt.uint8), ["qmb"], (), "dmb")
     S(act(T.ysb[:], T.pa[:, 0:C]), ["pa"], ["ysb"])
     load("s", T.y[:], T.ysb[:], ["ysb"], (), "dy")

@@ -4,10 +4,33 @@ C, M, VISITS = 256, 512, 3
 X4, U8, BF, F32, U16, I32 = "float8_e4m3fn_x4", "uint8", "bfloat16", "float32", "uint16", "int32"
 BIG, BASE = 16384.0, 4194304.0
 SHIFTS = 8
-GV = (20, 28, 28)
-LAST = 36
 H = C // 2
 EW = 516
+GV0 = 24
+GV = {1: (12, 10), 2: (12, 10)}
+LOOK = {1: "vs", 2: "vs"}
+COPY = {0: ('ssvs',), 1: ('sssv', 'svsv'), 2: ('ssss', 'ssss')}
+WRITE = {0: 'ssss', 1: 'ssss', 2: 'ssssssss'}
+PARTS = {0: 1, 1: 1}
+ASPLIT = {0: 0, 1: 1}
+LAST = ((0, 64, 40), (64, 128, 38))
+STORES = ((0, 64), (64, 128))
+YSPLIT = 0
+YBANK = ('pr0', 'pr1')
+YCOPY = 'ss'
+YQ = 'ss'
+OQ = 'yyyyy'
+SQ = 'yyys'
+ORDER = [6, 1, 0, 2, 3, 4, 9, 5, 24, 23, 21, 20, 7, 22, 10, 25, 8, 17, 29, 11, 36, 30, 37, 38, 15, 32, 12, 34, 35, 28, 18, 33, 27, 16, 13, 26, 41, 58, 14, 19, 45,
+         54, 59, 39, 31, 43, 60, 42, 61, 51, 62, 52, 64, 40, 65, 66, 53, 56, 82, 68, 49, 81, 44, 67, 71, 63, 57, 69, 85, 89, 77, 90, 70, 50, 74, 86, 83, 78, 88,
+         84, 75, 87, 79, 72, 76, 73, 55, 46, 80, 48, 91, 98, 101, 92, 102, 93, 94, 113, 103, 95, 104, 97, 105, 106, 111, 96, 126, 107, 109, 117, 112, 108, 115,
+         134, 118, 125, 47, 130, 100, 119, 110, 128, 120, 99, 114, 127, 121, 129, 122, 123, 133, 124, 132, 131, 162, 143, 116, 135, 144, 155, 145, 163, 136, 146,
+         137, 147, 138, 152, 158, 164, 149, 139, 165, 148, 140, 159, 141, 166, 156, 142, 150, 168, 151, 171, 167, 174, 157, 160, 153, 177, 154, 172, 175, 173,
+         169, 176, 178, 161, 170, 179, 181, 184, 180, 185, 183, 186, 196, 187, 198, 188, 194, 202, 190, 189, 203, 210, 200, 211, 197, 191, 213, 218, 217, 201,
+         192, 219, 193, 212, 195, 216, 214, 215, 199, 204, 182, 220, 205, 221, 222, 206, 223, 243, 224, 207, 234, 225, 226, 208, 227, 209, 228, 247, 248, 229,
+         249, 230, 259, 250, 251, 240, 237, 232, 256, 253, 262, 231, 252, 285, 260, 257, 261, 254, 286, 263, 233, 255, 264, 287, 235, 258, 238, 288, 244, 239,
+         241, 265, 236, 289, 245, 267, 277, 283, 242, 290, 281, 278, 279, 246, 284, 291, 282, 266, 271, 280, 269, 292, 275, 270, 273, 268, 272, 298, 274, 276,
+         299, 293, 300, 301, 294, 295, 302, 296, 308, 306, 297, 303, 307, 311, 309, 310, 304, 312, 305]
 
 
 def _sb(n, d):
@@ -25,7 +48,7 @@ SCRATCH = {
     "v1": _sb(64, F32), "v2": _sb(64, F32),
     "rs1": _sb(16, U16), "rs2": _sb(16, U16), "ra1": _sb(16, U16), "ra2": _sb(16, U16),
     "oa0": _sb(16, U16), "os1": _sb(16, U16), "os2": _sb(16, U16), "oa1": _sb(16, U16), "oa2": _sb(16, U16),
-    "tab": _sb(M + 256, F32), "val": _sb(VISITS * C, F32), "scan": _sb(M, F32), "moff": _sb(128, U16),
+    "tab": _sb(M + 256, F32), "val": _sb(VISITS * C, F32), "scan": _sb(C, F32), "mscan": _sb(M, F32), "moff": _sb(128, U16),
     "mc": _sb(4 * M, BF), "look": _sb(C, F32), "seq": _sb(C, F32),
     "c64": _sb(EW, BF), "ident": _sb(128, BF), "et": _sb(2 * EW, BF), "eq": _sb(512, X4), "es": _sb(512, U8),
     "kt": _sb(1536, BF), "kq": _sb(384, X4), "ks": _sb(384, U8),
@@ -35,9 +58,11 @@ SCRATCH = {
     "pa": ("psum", [128, 512], F32), "po": ("psum", [128, 512], F32), "pc": ("psum", [128, 512], F32), "ps": ("psum", [128, 512], F32),
     "pr0": ("psum", [128, 512], F32), "pr1": ("psum", [128, 512], F32), "pr2": ("psum", [128, 512], F32), "pr3": ("psum", [128, 512], F32),
 }
-DMAS = ["dx", "du", "dm", "dws", "dwa", "dwb", "dy", "dsc", "dma", "dmb", "ds0", "ds1", "ds2", "ds3"]
-SEMAPHORES = ["qv", "qs", "qt", "qg", "arr1", "arr2", "arr3", "arr3c", "ar1", "ar2", "ao1", "ao2", "sent"] + DMAS
+DMAS = ["dx", "du", "dm", "dws", "dwa", "dwb", "dy0", "dy1", "dsc", "dm0", "dm1", "dm2", "dm3", "ds0", "ds1", "ds2", "ds3"]
+SEMAPHORES = ["qv", "qs", "qt", "qg", "arr1", "arr2", "arr3", "ar10", "ar20", "ar11", "ar21", "ao1", "ao2",
+              "arc10", "arc11", "arc20", "arc21", "arc30", "arc31", "arr3a", "arr3b", "sent"] + DMAS
 PSUM = ("pa", "po", "pc", "ps", "pr0", "pr1", "pr2", "pr3")
+SETS = (("pr0", "pr1", "pr2", "pr3"), ("pa", "po", "pc", "ps"))
 
 
 def rank_program(g, core, T, topo):
@@ -51,7 +76,7 @@ def rank_program(g, core, T, topo):
 
     def op(q, fn, reads=(), writes=(), dma=None, after=()):
         me = len(ops)
-        deps = set()
+        deps, behind = set(), set()
         for k in reads:
             if k not in PSUM and k in writer:
                 deps.add(writer[k])
@@ -63,16 +88,18 @@ def rank_program(g, core, T, topo):
                     deps.add(d)
         for k in list(reads) + list(writes):
             if k in PSUM:
-                for q2, d in bank.setdefault(k, {}).items():
-                    if q2 != q:
+                for d in bank.setdefault(k, []):
+                    if ops[d]["q"] != q:
                         deps.add(d)
-                bank[k][q] = me
+                    elif q == "t":
+                        behind.add(d)
+                bank[k].append(me)
         for k in reads:
             readers.setdefault(k, []).append(me)
         for k in writes:
             writer[k] = me
             readers[k] = []
-        ops.append({"q": q, "fn": fn, "deps": deps, "dma": dma, "after": list(after), "need": False})
+        ops.append({"q": q, "fn": fn, "deps": deps, "behind": behind, "dma": dma, "after": list(after), "need": False})
 
     def V(fn, r=(), w=(), **k):
         op("v", fn, r, w, **k)
@@ -162,28 +189,18 @@ def rank_program(g, core, T, topo):
         S(act(T.kt[:, 1024 + t:1536:4], T.kt[:, 1024:1536:4]), ["kd0"], ["kd%d" % t])
     S(act(T.tab[:, 0:C], T.seq[:]), ["seq"], ["tab"])
     S(act(T.tab[:, C:M], T.seq[:], bias=float(4 * C)), ["seq"], ["tabb"])
-
-    def values(t):
+    for t in range(VISITS):
         S(act(T.val[:, C * t:C * t + C], T.seq[:], bias=float(4 * M + 4 * C * t)), ["seq"], ["val%d" % t])
-
-    def pack_e(b):
+    for b in range(4):
         a = EW * (b % 2) + 2 - 2 * (b // 2)
         V(qz(T.eq[:, 128 * b:128 * b + 128], T.es[:, 128 * b:128 * b + 128], T.et[:, a:a + 512]), ["et%d" % (b % 2)], ["eq%d" % b])
-
-    def pack_k():
-        V(qz(T.kq[:, 128:384], T.ks[:, 128:384], T.kt[:, 512:1536]), ["kc%d" % t for t in range(4)] + ["kd%d" % t for t in range(4)], ["kq1"])
-
-    def late_constants(i):
-        if i == 0:
-            V(ts(T.t4[:], T.i4[:, 0:4], tau, 1.0 / BASE, Alu.is_le, Alu.max), ["i4", "cf"], ["t4"])
-            V(ts(T.kscan[:], T.i4[:], tau, BASE, Alu.is_gt, Alu.mult), ["i4", "cf"], ["kscan"])
-            V(lambda: v.tensor_reduce(scol, T.t4[:], AxisListType.X, Alu.mult), ["t4"], ["scol"])
-        else:
-            V(ts(scol4, scol, 0.25, None, Alu.mult), ["scol"], ["scol4"])
-
+    V(qz(T.kq[:, 128:384], T.ks[:, 128:384], T.kt[:, 512:1536]), ["kc%d" % t for t in range(4)] + ["kd%d" % t for t in range(4)], ["kq1"])
+    V(ts(T.t4[:], T.i4[:, 0:4], tau, 1.0 / BASE, Alu.is_le, Alu.max), ["i4", "cf"], ["t4"])
+    V(ts(T.kscan[:], T.i4[:], tau, BASE, Alu.is_gt, Alu.mult), ["i4", "cf"], ["kscan"])
+    V(lambda: v.tensor_reduce(scol, T.t4[:], AxisListType.X, Alu.mult), ["t4"], ["scol"])
+    V(ts(scol4, scol, 0.25, None, Alu.mult), ["scol"], ["scol4"])
     V(qz(T.aq[:, 192:192 + C], T.aqs[:, 192:192 + C], T.xt[:]), ["xt"], ["state0"])
 
-    banks = [T.pr0, T.pr1, T.pr2, T.pr3]
     engines = [0]
 
     def kside(j):
@@ -198,9 +215,8 @@ def rank_program(g, core, T, topo):
     def work(a):
         return T.aq[:, a:a + 128], T.aqs[:, a:a + 128]
 
-    def map_offsets(a, z, key):
-        V(scan(T.scan[:, 4 * a:4 * z], T.tab[:, 4 * a:4 * z], 4 * (z - a)), ["kscan", "tab", "tabb"], ["scan" + key])
-        V(ts(T.moff[:, a:z], T.scan[:, 4 * a + 3:4 * z:4], scol, bcol, Alu.mult, Alu.add), ["scan" + key, "scol", "cf"], ["moff" + key])
+    def words(c, a, z):
+        return c[:, a:z].bitcast(dt.uint8)
 
     def gather(q, out, win, offs, reads, key, after=()):
         if q == "v":
@@ -217,202 +233,170 @@ def rank_program(g, core, T, topo):
     before = len(topo.engines(T.cores[(rank - 1) % n], core))
     home = len(topo.engines(T.cores[(rank + VISITS - 1) % n], core))
 
-    def product_a(c, sc, keys):
-        P(mm(T.pa[:, 0:C], T.uq[:], T.usq[:], c, sc, True, True), keys + ["uq"], ["pa"])
+    def scaled(q, out, in_, name, key):
+        if q == "s":
+            S(act(out, in_, 0.015625), [name], [key])
+        else:
+            V(ts(out, in_, 0.015625, None, Alu.mult), [name], [key])
 
-    def bits():
-        V(ts(T.wk[:, 0:C], T.pa[:, 0:C], 0.0, pw, Alu.is_gt, Alu.mult), ["pa", "pw"], ["bits"])
+    def addresses(c, sc, keys, a, z, pa, sums):
+        P(mm(T[pa][:, 0:z - a], T.uq[:], T.usq[:], c[:, a:z], sc[:, a:z], True, True), keys + ["uq"], [pa])
+        mine = ["bits%d" % h for h in range(a // H, z // H)]
+        V(ts(T.wk[:, a:z], T[pa][:, 0:z - a], 0.0, pw, Alu.is_gt, Alu.mult), [pa, "pw"], mine)
+        if sums:
+            V(qz(T.aq[:, 0:128], T.aqs[:, 0:128], T.wk[:, 0:512]), ["bits0", "bits1"] + fls[:4], ["bitq", "flq0"])
+        for j, name in sums:
+            P(mm(T[name][:, 0:128], *kside(j), *work(0), True, True), ["kq%d" % j, "bitq", "flq0"], [name])
 
-    def pack_bits():
-        V(qz(T.aq[:, 0:128], T.aqs[:, 0:128], T.wk[:, 0:512]), ["bits"] + fls[:4], ["bitq", "flq0"])
+    def send_addresses(t, a, z, pc):
+        name, h = "rs%d" % t, a // H
+        V(scan(T.v1[:, a // 4:z // 4], T[pc][:, a // 4:z // 4], (z - a) // 4), ["kscan", pc], ["v1%d" % h])
+        V(ts(T[name][:, a // 16:z // 16], T.v1[:, a // 4 + 3:z // 4:4], scol4, None, Alu.mult), ["v1%d" % h, "scol4"], [name + str(h)])
+        hop(T["ra%d" % t][:, a // 16:z // 16], T[name][:, a // 16:z // 16], "ar%d%d" % (t, h), nxt, [name + str(h)])
 
-    def sums(j):
-        P(mm((T.po, T.pc)[j][:, 0:128], *kside(j), *work(0), True, True), ["kq%d" % j, "bitq", "flq0"], [("po", "pc")[j]])
-
-    def owns():
+    def slots(t):
         S(act(T.own0[:], T.po[:, 0:64], bias=ge), ["po", "ge"], ["own0"])
         S(act(T.own[:], T.po[:, 0:64]), ["po"], ["own"])
-
-    def compare(j):
-        a = C + 256 * (j // 4)
-        o = "own" if j else "own0"
-        V(lambda: v.tensor_tensor(T.wk[:, a + 4 * j + j % 4:a + 256:4], T.pc[:, 0:64 - j], T[o][:, j:64], Alu.is_equal), ["pc", o], ["fl%d" % j])
-
-    def pack_flags():
+        for j in range(SHIFTS):
+            a = C + 256 * (j // 4)
+            o = "own" if j else "own0"
+            V(lambda j=j, a=a, o=o: v.tensor_tensor(T.wk[:, a + 4 * j + j % 4:a + 256:4], T.pc[:, 0:64 - j], T[o][:, j:64], Alu.is_equal), ["pc", o], ["fl%d" % j])
         V(qz(T.aq[:, 64:192], T.aqs[:, 64:192], T.wk[:, C:768]), fls, ["flq0", "flq1"])
-
-    def flags():
         P(mm(T.ps[:, 0:128], *kside(1), *work(0), True, False), ["kq1", "bitq", "flq0"], ["ps"])
         P(mm(T.ps[:, 0:128], *kside(2), *work(64), False, False), ["kq1", "flq0", "flq1"], ["ps"])
         P(mm(T.ps[:, 0:128], *kside(2), *work(128), False, True), ["kq1", "flq1", "state0"], ["ps"])
-
-    def slots_scan():
         V(scan(T.v2[:], T.ps[:, 0:64], 64), ["kscan", "ps"], ["v2"])
-
-    def slots(t):
         name = "os%d" % t if t else "oa0"
         for h in range(2):
             V(ts(T[name][:, h:16:2], T.v2[:, 3 + 4 * h:64:8], scol4, T.spare[:, h:h + 1], Alu.mult, Alu.min), ["v2", "scol4", "spare"], [name + "ab"[h]])
         if t:
             hop(T["oa%d" % t][:], T[name][:], "ao%d" % t, nxt, [name + "a", name + "b"])
 
-    def scatter(t, k):
-        V(lambda: v.tensor_copy(T.tab[:].indirect(T["oa%d" % t][:, 2 * k:2 * k + 2]), T.val[:, C * t + 32 * k:C * t + 32 * k + 32]),
-          ["oa0a", "oa0b", "val%d" % t], ["tab", "tabb"], after=[("ao%d" % t, before)] if t else [])
-
-    def unpack(b, c, sc, keys, start, stop):
-        P(mm(banks[b][:, 0:C], *eside(b), c, sc, start, stop), keys + ["eq%d" % b], ["pr%d" % b])
-
-    def scaled(q, out, b, key):
-        if q == "s":
-            S(act(out, banks[b][:, 0:C], 0.015625), ["pr%d" % b], [key])
-        else:
-            V(ts(out, banks[b][:, 0:C], 0.015625, None, Alu.mult), ["pr%d" % b], [key])
-
     for t in range(VISITS):
-        sc_, ss_ = (T["l%dc" % t][:], T["l%ds" % t][:]) if t else (T.aq[:, 192:192 + C], T.aqs[:, 192:192 + C])
+        sc_, ss_ = (T["l%dc" % t], T["l%ds" % t]) if t else (T.aq[:, 192:192 + C], T.aqs[:, 192:192 + C])
         yc, ys = T["y%dc" % t], T["y%ds" % t]
-        st = ["state0"] if t == 0 else []
         final = t + 1 == VISITS
         lo = 4 * M + 4 * C * t
-        yq = ["yq%d" % t]
-        pk = ["pool_m"] + ["pool%d_%d" % (a, b) for a in range(t) for b in range(4)]
-        gv = 16 * GV[t]
-
-        def layer(b, start, stop):
-            P(mm(banks[b][:, 0:C], *wside(b), sc_, ss_, start, stop), st + ["w%d" % b, "ws"], ["pr%d" % b], after=[("arr%d" % t, 2 * before)] if t else [])
-
-        def written(b, q="s"):
-            unpack(b, yc[:], ys[:], yq, True, True)
-            scaled(q, T.pool[:, lo + b:lo + 4 * C:4], b, "pool%d_%d" % (t, b))
-
-        def read_b():
-            gather("s", T.bt[:, gv:4 * C], T.pool[:, 0:lo], T.off[:, GV[t]:64], pk + ["off"], "btb")
-            gather("v", T.bt[:, 0:gv], T.pool[:, 0:lo], T.off[:, 0:GV[t]], pk + ["off"], "bta")
-
-        def pack_b():
-            V(qz(T.bq[:], T.bs[:], T.bt[:]), ["bta", "btb"], ["bq"])
+        pk = ["pool_m"] + ["pool%d_%d%s" % (a, b, x) for a in range(t) for b in range(4) for x in ("", "x")]
+        yq = ["yq%d0" % t, "yq%d1" % t]
+        dst = T.cores[(rank - VISITS + 1) % n] if final else nxt
+        land = T["l%dc" % (t + 1)]
 
         if t == 0:
-            product_a(sc_, ss_, st)
-            pack_k()
-            bits()
-            pack_bits()
-            sums(0)
-            sums(1)
-            pack_e(0)
-            V(ts(T.off[:], T.po[:, 0:64], bcol, None, Alu.add), ["po", "cf"], ["off"])
-            pack_e(2)
-            read_b()
-            owns()
-            values(0)
-            pack_e(1)
-            pack_e(3)
-            late_constants(0)
-            pack_b()
-            layer(0, True, False)
-            layer(1, True, False)
+            P(mm(T.pa[:, 0:C], T.uq[:], T.usq[:], sc_, ss_, True, True), ["state0", "uq"], ["pa"])
+            V(ts(T.wk[:, 0:C], T.pa[:, 0:C], 0.0, pw, Alu.is_gt, Alu.mult), ["pa", "pw"], ["bits0", "bits1"])
+            V(qz(T.aq[:, 0:128], T.aqs[:, 0:128], T.wk[:, 0:512]), ["bits0", "bits1"] + fls[:4], ["bitq", "flq0"])
+            for j, name in ((0, "po"), (1, "pc")):
+                P(mm(T[name][:, 0:128], *kside(j), *work(0), True, True), ["kq%d" % j, "bitq", "flq0"], [name])
+            V(ts(T.off[:], T.po[:, 0:64], bcol, None, Alu.add), ["po", "cf"], ["off0", "off1"])
+            gather("s", T.bt[:, 16 * GV0:4 * C], T.pool[:, 0:lo], T.off[:, GV0:64], pk + ["off0", "off1"], "bts0")
+            gather("v", T.bt[:, 0:16 * GV0], T.pool[:, 0:lo], T.off[:, 0:GV0], pk + ["off0", "off1"], "btv0")
+            V(qz(T.bq[:], T.bs[:], T.bt[:]), ["bts0", "btv0", "bts1", "btv1"], ["bq0", "bq1"])
             for b in range(4):
-                unpack(b, T.bq[:], T.bs[:], ["bq"], b > 1, b < 2)
-            layer(2, False, True)
-            layer(3, False, True)
-            late_constants(1)
-            for j in range(4):
-                compare(j)
+                name = SETS[0][b]
+                calls = [(mm(T[name][:, 0:C], *wside(b), sc_, ss_, b < 2, b > 1), ["state0", "w%d" % b, "ws"]),
+                         (mm(T[name][:, 0:C], *eside(b), T.bq[:], T.bs[:], b > 1, b < 2), ["bq0", "bq1", "eq%d" % b])]
+                for fn, keys in (calls if b < 2 else calls[::-1]):
+                    P(fn, keys, [name])
+                scaled(COPY[0][0][b], T.yt[:, b:4 * C:4], T[name][:, 0:C], name, "yt0%d" % b)
+            V(qz(yc[:], ys[:], T.yt[:]), ["yt%d%d" % (h, b) for h in range(2) for b in range(4)], yq)
+            slots(0)
         else:
-            lists = [("ar%d" % t, before)]
-            gather("s", T.look[:, H:C], T.tab[:, 0:M], T["ra%d" % t][:, 8:16], ["tab", "tabb"], "lookb", after=lists)
-            gather("v", T.look[:, 0:H], T.tab[:, 0:M], T["ra%d" % t][:, 0:8], ["tab", "tabb"], "looka", after=lists)
-            for b in range(4):
-                layer(b, True, False)
-            V(scan(T.scan[:, 0:C], T.look[:], C), ["kscan", "looka", "lookb"], ["scana"])
-            slots_scan()
-            V(ts(T.off[:], T.scan[:, 3:C:4], scol, bcol, Alu.mult, Alu.add), ["scana", "scol", "cf"], ["off"])
-            read_b()
-            slots(t)
-            pack_b()
-            for b in range(4):
-                unpack(b, T.bq[:], T.bs[:], ["bq"], False, True)
-        for b in range(4):
-            scaled("sv"[b % 2], T.yt[:, b:4 * C:4], b, "yt%d" % b)
-            if t == 0 and b == 1:
-                for j in range(4, 8):
-                    compare(j)
-                pack_flags()
-                flags()
-        V(qz(yc[:], ys[:], T.yt[:]), ["yt%d" % b for b in range(4)], yq)
+            parts = PARTS[t - 1]
+            for h in range(2):
+                a, z, gv = H * h, H * h + H, GV[t][h]
+                gather(LOOK[t][h], T.look[:, a:z], T.tab[:, 0:M], T["ra%d" % t][:, 8 * h:8 * h + 8], ["tab", "tabb"], "look%d" % h,
+                       after=[("ar%d%d" % (t, h if parts > 1 else 0), before)])
+                V(scan(T.scan[:, a:z], T.look[:, a:z], H), ["kscan", "look%d" % h], ["scan%d" % h])
+                V(ts(T.off[:, 32 * h:32 * h + 32], T.scan[:, a + 3:z:4], scol, bcol, Alu.mult, Alu.add), ["scan%d" % h, "scol", "cf"], ["off%d" % h])
+                gather("s", T.bt[:, 4 * a + 16 * gv:4 * z], T.pool[:, 0:lo], T.off[:, 32 * h + gv:32 * h + 32], pk + ["off%d" % h], "bts%d" % h)
+                if gv:
+                    gather("v", T.bt[:, 4 * a:4 * a + 16 * gv], T.pool[:, 0:lo], T.off[:, 32 * h:32 * h + gv], pk + ["off%d" % h], "btv%d" % h)
+                V(qz(T.bq[:, a:z], T.bs[:, a:z], T.bt[:, 4 * a:4 * z]), ["bts%d" % h, "btv%d" % h], ["bq%d" % h])
+                for b in range(4):
+                    name = SETS[h][b]
+                    P(mm(T[name][:, 0:H], *wside(b), sc_[:, a:z], ss_[:, a:z], True, False), ["w%d" % b, "ws"], [name],
+                      after=[("arr%d" % t, before), ("arc%d%d" % (t, h), before)])
+                    P(mm(T[name][:, 0:H], *eside(b), T.bq[:, a:z], T.bs[:, a:z], False, True), ["bq%d" % h, "eq%d" % b], [name])
+                    scaled(COPY[t][h][b], T.yt[:, 4 * a + b:4 * z:4], T[name][:, 0:H], name, "yt%d%d" % (h, b))
+                V(qz(yc[:, a:z], ys[:, a:z], T.yt[:, 4 * a:4 * z]), ["yt%d%d" % (h, b) for b in range(4)], [yq[h]])
+        for h in range(2):
+            hop(words(land, H * h, H * h + H), words(yc, H * h, H * h + H), "arc%d%d" % (t + 1, h), dst, [yq[h]])
+        if final and YSPLIT:
+            for h in range(2):
+                hop(T.fins[:, H * h:H * h + H], ys[:, H * h:H * h + H], "arr3" + "ab"[h], dst, [yq[h]])
+        else:
+            hop(T.fins[:, 0:C] if final else T["l%ds" % (t + 1)][:], ys[:], "arr%d" % (t + 1), dst, yq)
         if not final:
-            hop(T["l%dc" % (t + 1)][:].bitcast(dt.uint8), yc[:].bitcast(dt.uint8), "arr%d" % (t + 1), nxt, yq)
-            product_a(yc[:], ys[:], yq)
-            if t == 0:
-                slots_scan()
-                slots(0)
+            if PARTS[t] == 1 and ASPLIT[t]:
+                addresses(yc, ys, yq[:1], 0, H, "pr0", ())
+                addresses(yc, ys, yq[1:], H, C, "pa", ((1, "pc"), (0, "po")))
+                send_addresses(t + 1, 0, C, "pc")
+            elif PARTS[t] == 1:
+                addresses(yc, ys, yq, 0, C, "pa", ((1, "pc"), (0, "po")))
+                send_addresses(t + 1, 0, C, "pc")
             else:
-                scatter(t, 7)
-            bits()
-            written(0)
-            pack_bits()
-            sums(1)
-            sums(0)
-            scatter(t, 6 if t else 7)
-            name = "rs%d" % (t + 1)
-            V(scan(T.v1[:], T.pc[:, 0:64], 64), ["kscan", "pc"], ["v1"])
-            V(ts(T[name][:], T.v1[:, 3:64:4], scol4, None, Alu.mult), ["v1", "scol4"], [name])
-            hop(T["ra%d" % (t + 1)][:], T[name][:], "ar%d" % (t + 1), nxt, [name])
-            hop(T["l%ds" % (t + 1)][:], ys[:], "arr%d" % (t + 1), nxt, yq)
-            owns()
-            for b in range(1, 4):
-                written(b)
-            values(t + 1)
-            for j in range(SHIFTS):
-                k = (5 if t else 6) - j
-                if k >= 0:
-                    scatter(t, k)
-                compare(j)
-            pack_flags()
-            flags()
-        else:
-            dst = T.cores[(rank - VISITS + 1) % n]
-            hop(T.l3c[:].bitcast(dt.uint8), yc[:].bitcast(dt.uint8), "arr3c", dst, yq)
-            hop(T.fins[:, 0:C], ys[:], "arr3", dst, yq)
+                addresses(yc, ys, yq[:1], 0, H, "pr0", ((1, "pr1"),))
+                send_addresses(t + 1, 0, H, "pr1")
+                addresses(yc, ys, yq[1:], H, C, "pa", ((1, "pc"), (0, "po")))
+                send_addresses(t + 1, H, C, "pc")
+        for h, (a, z) in enumerate(((0, H), (H, C)) if len(WRITE[t]) == 8 else ((0, C),)):
             for b in range(4):
-                written(b)
-            for k in range(7, -1, -1):
-                scatter(t, k)
-            pk = pk + ["pool%d_%d" % (t, b) for b in range(4)]
-            mc, pwin = T.mc, T.pool[:, 0:lo + 4 * C]
-            map_offsets(0, 64, "a")
-            map_offsets(64, 128, "b")
-            for a, key in ((0, "a"), (64, "b")):
-                gather("s", mc[:, 16 * a:16 * (a + LAST)], pwin, T.moff[:, a:a + LAST], pk + ["moff" + key], "ms" + key)
-                gather("v", mc[:, 16 * (a + LAST):16 * (a + 64)], pwin, T.moff[:, a + LAST:a + 64], pk + ["moff" + key], "mv" + key)
-                V(qz(T.qmc[:, 4 * a:4 * a + C], T.fins[:, C + 4 * a:2 * C + 4 * a], mc[:, 16 * a:16 * a + 4 * C]), ["ms" + key, "mv" + key], ["qm" + key])
+                name = SETS[h if final else 0][(b + 2) % 4]
+                P(mm(T[name][:, 0:z - a], *eside(b), yc[:, a:z], ys[:, a:z], True, True), yq[a // H:z // H] + ["eq%d" % b], [name])
+                scaled(WRITE[t][4 * h + b], T.pool[:, lo + 4 * a + b:lo + 4 * z:4], T[name][:, 0:z - a], name, "pool%d_%d%s" % (t, b, "x" * h))
+        for k in range(7, -1, -1):
+            V(lambda k=k, t=t: v.tensor_copy(T.tab[:].indirect(T["oa%d" % t][:, 2 * k:2 * k + 2]), T.val[:, C * t + 32 * k:C * t + 32 * k + 32]),
+              ["oa0a", "oa0b", "val%d" % t], ["tab", "tabb"], after=[("ao%d" % t, before)] if t else [])
+        if not final:
+            slots(t + 1)
 
-    codes, both = [("arr3c", home)], [("arr3c", home), ("arr3", home)]
-    P(mm(T.pa[:, 0:C], *wside(0), T.l3c[:], T.fins[:, 0:C], True, True), ["w0", "ws"], ["pa"], after=both)
-    load("y", T.oc[:, 0:4 * C], T.l3c[:].bitcast(dt.uint8), (), (), "dsc", after=codes)
-    load("y", T.oc[:, 4 * C:8 * C], T.qmc[:, 0:C].bitcast(dt.uint8), ["qma"], (), "dma")
-    load("y", T.oc[:, 8 * C:12 * C], T.qmc[:, C:2 * C].bitcast(dt.uint8), ["qmb"], (), "dmb")
-    S(act(T.ysb[:], T.pa[:, 0:C]), ["pa"], ["ysb"])
-    load("s", T.y[:], T.ysb[:], ["ysb"], (), "dy")
+    pk = pk + ["pool%d_%d%s" % (VISITS - 1, b, x) for b in range(4) for x in ("", "x")]
+    for a, z, share in LAST:
+        key = str(a)
+        V(scan(T.mscan[:, 4 * a:4 * z], T.tab[:, 4 * a:4 * z], 4 * (z - a)), ["kscan", "tab", "tabb"], ["mscan" + key])
+        V(ts(T.moff[:, a:z], T.mscan[:, 4 * a + 3:4 * z:4], scol, bcol, Alu.mult, Alu.add), ["mscan" + key, "scol", "cf"], ["moff" + key])
+        gather("s", T.mc[:, 16 * a:16 * (a + share)], T.pool[:], T.moff[:, a:a + share], pk + ["moff" + key], "ms" + key)
+        if a + share < z:
+            gather("v", T.mc[:, 16 * (a + share):16 * z], T.pool[:], T.moff[:, a + share:z], pk + ["moff" + key], "mv" + key)
+        V(qz(T.qmc[:, 4 * a:4 * z], T.fins[:, C + 4 * a:C + 4 * z], T.mc[:, 16 * a:16 * z]), ["ms" + key, "mv" + key], ["qm" + key])
+
+    codes = [("arc30", home), ("arc31", home)]
+    planes = [("arr3a", home), ("arr3b", home)] if YSPLIT else [("arr3", home)]
+    qm = ["qm%d" % a for a, z, share in LAST]
+    for h, (a, z) in enumerate(((0, H), (H, C)) if YSPLIT else ((0, C),)):
+        name = YBANK[h]
+        P(mm(T[name][:, 0:z - a], *wside(0), T.l3c[:, a:z], T.fins[:, a:z], True, True), ["w0", "ws"], [name],
+          after=[codes[h], planes[h]] if YSPLIT else codes + planes)
+        if YCOPY[h] == "s":
+            S(act(T.ysb[:, a:z], T[name][:, 0:z - a]), [name], ["ysb%d" % h])
+        else:
+            V(lambda a=a, z=z, name=name: v.tensor_copy(T.ysb[:, a:z], T[name][:, 0:z - a]), [name], ["ysb%d" % h])
+        load(YQ[h], T.y[:, a:z], T.ysb[:, a:z], ["ysb%d" % h], (), "dy%d" % h)
+    load(OQ[0], T.oc[:, 0:4 * C], T.l3c[:].bitcast(dt.uint8), (), (), "dsc", after=codes)
+    for h, (a, z) in enumerate(STORES):
+        load(OQ[1 + h], T.oc[:, 4 * C + 16 * a:4 * C + 16 * z], words(T.qmc, 4 * a, 4 * z), ["qm%d" % a2 for a2, z2, share in LAST if a <= a2 < z], (), "dm%d" % h)
     for k in range(4):
-        load("y" if k < 3 else "s", T.osc[4 * k:4 * k + 4, :], T.fins[32 * k:32 * k + 4, :], ["qma", "qmb"], (), "ds%d" % k, after=both[1:])
+        load(SQ[k], T.osc[4 * k:4 * k + 4, :], T.fins[32 * k:32 * k + 4, :], qm, (), "ds%d" % k, after=planes)
 
+    order = ORDER or list(range(len(ops)))
+    place = {d: i for i, d in enumerate(order)}
     last = {}
-    for o in ops:
-        best = {}
+    for me in order:
+        o, best = ops[me], {}
         for d in o["deps"]:
-            p = ops[d]
-            key = p["dma"] or p["q"]
-            best[key] = max(best.get(key, -1), d)
+            key = ops[d]["dma"] or ops[d]["q"]
+            if key not in best or place[best[key]] < place[d]:
+                best[key] = d
         o["deps"] = []
         for key, d in best.items():
-            if last.get((o["q"], key), -1) < d:
-                last[(o["q"], key)] = d
+            if last.get((o["q"], key), -1) < place[d]:
+                last[(o["q"], key)] = place[d]
                 ops[d]["need"] = True
                 o["deps"].append(d)
     count, seen = {}, set()
-    for o in ops:
+    for me in order:
+        o = ops[me]
         q = o["q"]
         for name, val in o["after"]:
             if (q, name) not in seen:
@@ -431,7 +415,6 @@ def rank_program(g, core, T, topo):
             o["sem"], o["val"] = counter[q], count[q]
             ins.then_inc(T.sem[counter[q]], 1)
     g.wait_ge(T.sem.sent, engines[0])
-    for name in ("dma", "dsc", "dmb", "ds0", "ds1", "ds2"):
-        g.sync.wait_ge(T.sem[name], 16)
-    for name in ("dy", "ds3"):
-        s.wait_ge(T.sem[name], 16)
+    for o in ops:
+        if o["dma"] not in (None, "remote") and not o["need"]:
+            eng[o["q"]].wait_ge(T.sem[o["dma"]], 16)

@@ -5,32 +5,31 @@ X4, U8, BF, F32, U16, I32 = "float8_e4m3fn_x4", "uint8", "bfloat16", "float32", 
 BIG, BASE = 16384.0, 4194304.0
 SHIFTS = 8
 H = C // 2
-EW = 516
-GV0 = 24
-GV = {1: (12, 10), 2: (12, 10)}
+EW = 514
+GV = {0: (12, 10), 1: (12, 10), 2: (12, 10)}
 LOOK = {1: "vs", 2: "vs"}
-COPY = {0: ('ssvs',), 1: ('sssv', 'svsv'), 2: ('ssss', 'ssss')}
+COPY = {0: ('sssv', 'sssv'), 1: ('sssv', 'svsv'), 2: ('ssss', 'ssss')}
 WRITE = {0: 'ssss', 1: 'ssss', 2: 'ssssssss'}
-PARTS = {0: 1, 1: 1}
-ASPLIT = {0: 0, 1: 1}
-LAST = ((0, 64, 40), (64, 128, 38))
+BANKS = {0: ("pa", "po", "pr0", "pr1"), 1: ("pa", "po", "pc", "ps"), 2: ("pa", "po", "pc", "ps")}
+ABANK = {0: "pr2", 1: "pr0"}
+WA = 2
+LAST = ((0, 64, 38), (64, 128, 36))
 STORES = ((0, 64), (64, 128))
-YSPLIT = 0
-YBANK = ('pr0', 'pr1')
-YCOPY = 'ss'
-YQ = 'ss'
+YCOPY = 's'
+YQ = 's'
 OQ = 'yyyyy'
 SQ = 'yyys'
-ORDER = [6, 1, 0, 2, 3, 4, 9, 5, 24, 23, 21, 20, 7, 22, 10, 25, 8, 17, 29, 11, 36, 30, 37, 38, 15, 32, 12, 34, 35, 28, 18, 33, 27, 16, 13, 26, 41, 58, 14, 19, 45,
-         54, 59, 39, 31, 43, 60, 42, 61, 51, 62, 52, 64, 40, 65, 66, 53, 56, 82, 68, 49, 81, 44, 67, 71, 63, 57, 69, 85, 89, 77, 90, 70, 50, 74, 86, 83, 78, 88,
-         84, 75, 87, 79, 72, 76, 73, 55, 46, 80, 48, 91, 98, 101, 92, 102, 93, 94, 113, 103, 95, 104, 97, 105, 106, 111, 96, 126, 107, 109, 117, 112, 108, 115,
-         134, 118, 125, 47, 130, 100, 119, 110, 128, 120, 99, 114, 127, 121, 129, 122, 123, 133, 124, 132, 131, 162, 143, 116, 135, 144, 155, 145, 163, 136, 146,
-         137, 147, 138, 152, 158, 164, 149, 139, 165, 148, 140, 159, 141, 166, 156, 142, 150, 168, 151, 171, 167, 174, 157, 160, 153, 177, 154, 172, 175, 173,
-         169, 176, 178, 161, 170, 179, 181, 184, 180, 185, 183, 186, 196, 187, 198, 188, 194, 202, 190, 189, 203, 210, 200, 211, 197, 191, 213, 218, 217, 201,
-         192, 219, 193, 212, 195, 216, 214, 215, 199, 204, 182, 220, 205, 221, 222, 206, 223, 243, 224, 207, 234, 225, 226, 208, 227, 209, 228, 247, 248, 229,
-         249, 230, 259, 250, 251, 240, 237, 232, 256, 253, 262, 231, 252, 285, 260, 257, 261, 254, 286, 263, 233, 255, 264, 287, 235, 258, 238, 288, 244, 239,
-         241, 265, 236, 289, 245, 267, 277, 283, 242, 290, 281, 278, 279, 246, 284, 291, 282, 266, 271, 280, 269, 292, 275, 270, 273, 268, 272, 298, 274, 276,
-         299, 293, 300, 301, 294, 295, 302, 296, 308, 306, 297, 303, 307, 311, 309, 310, 304, 312, 305]
+ORDER = [0, 1, 6, 10, 2, 3, 9, 4, 5, 23, 17, 25, 21, 8, 22, 24, 7, 18, 26, 28, 34, 30, 36, 31, 37, 32, 15, 12, 41, 55, 35, 14, 38, 33, 40, 11, 39, 16, 27, 56, 13,
+         52, 42, 57, 19, 29, 20, 58, 51, 50, 59, 70, 53, 76, 61, 73, 48, 60, 64, 67, 65, 83, 49, 62, 63, 80, 66, 86, 54, 102, 68, 81, 71, 74, 69, 103, 77, 101,
+         72, 98, 75, 89, 82, 92, 97, 99, 90, 100, 84, 96, 78, 93, 91, 104, 87, 85, 79, 88, 105, 94, 43, 106, 111, 107, 95, 45, 114, 108, 44, 116, 115, 109, 117,
+         124, 110, 130, 118, 125, 132, 119, 131, 128, 133, 121, 120, 126, 134, 141, 122, 140, 135, 46, 123, 143, 129, 136, 142, 127, 137, 145, 47, 113, 147,
+         149, 138, 146, 139, 112, 148, 158, 177, 144, 159, 150, 160, 178, 161, 162, 170, 151, 152, 179, 153, 164, 180, 167, 154, 163, 173, 156, 155, 192, 181,
+         171, 157, 168, 174, 182, 165, 169, 183, 175, 172, 189, 166, 186, 187, 176, 190, 193, 188, 184, 191, 196, 199, 194, 185, 195, 200, 201, 197, 217, 202,
+         203, 218, 205, 204, 219, 213, 226, 206, 211, 228, 214, 233, 209, 207, 220, 225, 215, 208, 229, 210, 234, 227, 230, 216, 232, 231, 221, 198, 235, 222,
+         236, 237, 223, 238, 239, 224, 240, 241, 243, 262, 242, 212, 263, 244, 264, 245, 265, 266, 271, 268, 247, 249, 258, 246, 274, 252, 267, 277, 269, 275,
+         300, 278, 270, 248, 272, 276, 301, 279, 259, 273, 250, 302, 253, 260, 280, 255, 251, 256, 303, 254, 282, 298, 257, 296, 304, 294, 261, 295, 305, 299,
+         281, 286, 297, 284, 306, 290, 288, 285, 307, 292, 289, 283, 313, 293, 287, 291, 314, 308, 315, 309, 316, 310, 311, 321, 317, 312, 323, 318, 322, 325,
+         326, 324, 319, 327, 320]
 
 
 def _sb(n, d):
@@ -50,17 +49,17 @@ SCRATCH = {
     "oa0": _sb(16, U16), "os1": _sb(16, U16), "os2": _sb(16, U16), "oa1": _sb(16, U16), "oa2": _sb(16, U16),
     "tab": _sb(M + 256, F32), "val": _sb(VISITS * C, F32), "scan": _sb(C, F32), "mscan": _sb(M, F32), "moff": _sb(128, U16),
     "mc": _sb(4 * M, BF), "look": _sb(C, F32), "seq": _sb(C, F32),
-    "c64": _sb(EW, BF), "ident": _sb(128, BF), "et": _sb(2 * EW, BF), "eq": _sb(512, X4), "es": _sb(512, U8),
+    "c64": _sb(EW, BF), "ident": _sb(128, BF), "et": _sb(1026, BF), "eq": _sb(512, X4), "es": _sb(512, U8),
     "kt": _sb(1536, BF), "kq": _sb(384, X4), "ks": _sb(384, U8),
     "iq": _sb(1, I32), "ci": _sb(8, I32), "cf": _sb(8, F32), "col": _sb(8, F32), "i18": _sb(18, F32), "t18": _sb(18, F32),
-    "ia": _sb(128, BF), "ic": _sb(128, BF), "i4": _sb(C, BF), "t4": _sb(4, F32),
+    "ia": _sb(512, BF), "gm": _sb(32, BF), "ic": _sb(128, BF), "i4": _sb(C, BF), "t4": _sb(4, F32),
     "spare": _sb(2, F32), "kscan": _sb(C, BF), "ysb": _sb(C, F32),
     "pa": ("psum", [128, 512], F32), "po": ("psum", [128, 512], F32), "pc": ("psum", [128, 512], F32), "ps": ("psum", [128, 512], F32),
     "pr0": ("psum", [128, 512], F32), "pr1": ("psum", [128, 512], F32), "pr2": ("psum", [128, 512], F32), "pr3": ("psum", [128, 512], F32),
 }
-DMAS = ["dx", "du", "dm", "dws", "dwa", "dwb", "dy0", "dy1", "dsc", "dm0", "dm1", "dm2", "dm3", "ds0", "ds1", "ds2", "ds3"]
-SEMAPHORES = ["qv", "qs", "qt", "qg", "arr1", "arr2", "arr3", "ar10", "ar20", "ar11", "ar21", "ao1", "ao2",
-              "arc10", "arc11", "arc20", "arc21", "arc30", "arc31", "arr3a", "arr3b", "sent"] + DMAS
+DMAS = ["dx", "du", "dm", "dws", "dwa", "dwb", "dy", "dsc", "dm0", "dm1", "dm2", "dm3", "ds0", "ds1", "ds2", "ds3"]
+SEMAPHORES = ["qv", "qs", "qt", "qg", "arr1", "arr2", "arr3", "ar1", "ar2", "ao1", "ao2",
+              "arc10", "arc11", "arc20", "arc21", "arc30", "arc31", "sent"] + DMAS
 PSUM = ("pa", "po", "pc", "ps", "pr0", "pr1", "pr2", "pr3")
 SETS = (("pr0", "pr1", "pr2", "pr3"), ("pa", "po", "pc", "ps"))
 
@@ -148,12 +147,12 @@ def rank_program(g, core, T, topo):
     load("s", T.ut[:], T.u[:], (), ["ut"], "du")
     load("y", T.pool[:, 0:4 * M], T.m[:], (), ["pool_m"], "dm")
     load("y", T.wsq[:], T.ws[:], (), ["ws"], "dws")
-    load("y", T.wq[:, 0:256].bitcast(dt.uint8), T.wc[:, 0:1024], (), ["w0", "w1"], "dwa")
-    load("y", T.wq[:, 256:512].bitcast(dt.uint8), T.wc[:, 1024:2048], (), ["w2", "w3"], "dwb")
+    load("y", T.wq[:, 0:128 * WA].bitcast(dt.uint8), T.wc[:, 0:512 * WA], (), ["w%d" % b for b in range(WA)], "dwa")
+    load("y", T.wq[:, 128 * WA:512].bitcast(dt.uint8), T.wc[:, 512 * WA:2048], (), ["w%d" % b for b in range(WA, 4)], "dwb")
 
     fls = ["fl%d" % j for j in range(SHIFTS)]
     G(iota(T.iq[:], [[0, 1]], 0, 1, False), (), ["iq"])
-    G(iota(T.ia[:], [[4, 8], [1, 4], [0, 4]], 0, 0), (), ["ia"])
+    G(iota(T.ia[:], [[1, 32], [0, 4], [-1, 4]], 0, 0), (), ["ia"])
     G(iota(T.i18[:], [[1, 18]], -2, 0), (), ["i18"])
     G(iota(T.ic[:], [[4, 8], [0, 4], [1, 4]], 0, 0), (), ["ic"])
     V(lambda: v.memset(T.c64[:], 64.0), (), ["c64"])
@@ -161,11 +160,12 @@ def rank_program(g, core, T, topo):
     G(iota(T.i4[:], [[0, C // 4], [1, 4]], 0, 0), (), ["i4"])
     G(iota(T.seq[:], [[4, C]], 0, 0), (), ["seq"])
     G(iota(T.spare[:], [[128, 2]], M, 1), (), ["spare"])
-    for h in range(2):
-        S(act(T.et[:, EW * h:EW * h + EW], T.c64[:], 0.0), ["c64"], ["et%d" % h])
+    S(act(T.et[:, 0:EW], T.c64[:], 0.0), ["c64"], ["et0"])
+    S(act(T.et[:, EW:1026], T.c64[:, 0:512], 0.0), ["c64"], ["et1"])
+    S(act(T.kt[:, 512:1024], T.c64[:, 0:512], 0.0), ["c64"], ["kc%d" % t for t in range(4)])
     S(act(T.wk[:, C:768], T.c64[:, 0:512], 0.0), ["c64"], fls)
     for h in range(2):
-        S(act(T.et[:, EW * h + 2 + h:EW * h + 512 + h:4], T.ident[:]), ["ident"], ["et%d" % h])
+        S(act(T.et[:, 513 * h + 2:513 * h + 512:4], T.ident[:]), ["ident"], ["et%d" % h])
     V(ts(T.ci[:, 1:2], T.iq[:], 2, 28, Alu.logical_shift_right, Alu.bitwise_and), ["iq"], ["ci1"])
     V(ts(T.ci[:, 4:5], T.iq[:], 15, None, Alu.bitwise_and), ["iq"], ["ci4"])
     V(ts(T.ci[:, 0:1], T.iq[:], 2, None, Alu.logical_shift_right), ["iq"], ["ci0"])
@@ -174,16 +174,16 @@ def rank_program(g, core, T, topo):
     V(lambda: v.tensor_copy(T.cf[:, 0:5], T.ci[:, 0:5]), ["ci0", "ci1", "ci2", "ci3", "ci4"], ["cf"])
     q4, g4, tau, bcol, icol = [T.cf[:, j:j + 1] for j in range(5)]
     p2, pw, ge, scol, scol4 = [T.col[:, j:j + 1] for j in range(5)]
-    for t in range(4):
-        V(ts(T.kt[:, t:512:4], T.ia[:], float(t), g4, Alu.subtract, Alu.is_equal), ["ia", "cf"], ["ka%d" % t])
+    V(ts(T.kt[:, 0:512], T.ia[:], g4, None, Alu.is_equal), ["ia", "cf"], ["ka"])
     V(ts(T.t18[:], T.i18[:], icol, 1.0, Alu.is_lt, Alu.add), ["i18", "cf"], ["t18"])
-    V(qz(T.kq[:, 0:128], T.ks[:, 0:128], T.kt[:, 0:512]), ["ka%d" % t for t in range(4)], ["kq0"])
+    V(qz(T.kq[:, 0:128], T.ks[:, 0:128], T.kt[:, 0:512]), ["ka"], ["kq0"])
     V(lambda: v.tensor_reduce(p2, T.t18[:], AxisListType.X, Alu.mult), ["t18"], ["p2"])
     V(ts(T.kt[:, 1024:1536:4], T.ic[:], q4, BIG, Alu.is_equal, Alu.mult), ["ic", "cf"], ["kd0"])
     V(ts(pw, icol, 9.0, p2, Alu.is_lt, Alu.mult), ["cf", "p2"], ["pw"])
     V(qz(T.uq[:], T.usq[:], T.ut[:]), ["ut"], ["uq"])
+    V(ts(T.gm[:], T.ic[:, 0:128:4], g4, None, Alu.is_equal), ["ic", "cf"], ["gm"])
     for t in range(4):
-        V(ts(T.kt[:, 512 + t:1024:4], T.ic[:], float(t), g4, Alu.subtract, Alu.is_equal), ["ic", "cf"], ["kc%d" % t])
+        S(act(T.kt[:, 512 + 5 * t:1024:16], T.gm[:]), ["gm"], ["kc%d" % t])
     V(ts(ge, bcol, tau, BIG, Alu.is_ge, Alu.mult), ["cf"], ["ge"])
     for t in range(1, 4):
         S(act(T.kt[:, 1024 + t:1536:4], T.kt[:, 1024:1536:4]), ["kd0"], ["kd%d" % t])
@@ -191,9 +191,8 @@ def rank_program(g, core, T, topo):
     S(act(T.tab[:, C:M], T.seq[:], bias=float(4 * C)), ["seq"], ["tabb"])
     for t in range(VISITS):
         S(act(T.val[:, C * t:C * t + C], T.seq[:], bias=float(4 * M + 4 * C * t)), ["seq"], ["val%d" % t])
-    for b in range(4):
-        a = EW * (b % 2) + 2 - 2 * (b // 2)
-        V(qz(T.eq[:, 128 * b:128 * b + 128], T.es[:, 128 * b:128 * b + 128], T.et[:, a:a + 512]), ["et%d" % (b % 2)], ["eq%d" % b])
+    for h in range(2):
+        V(qz(T.eq[:, 256 * h:256 * h + 256], T.es[:, 256 * h:256 * h + 256], T.et[:, 2 - 2 * h:1026 - 2 * h]), ["et0", "et1"], ["eq%d" % (2 * h), "eq%d" % (2 * h + 1)])
     V(qz(T.kq[:, 128:384], T.ks[:, 128:384], T.kt[:, 512:1536]), ["kc%d" % t for t in range(4)] + ["kd%d" % t for t in range(4)], ["kq1"])
     V(ts(T.t4[:], T.i4[:, 0:4], tau, 1.0 / BASE, Alu.is_le, Alu.max), ["i4", "cf"], ["t4"])
     V(ts(T.kscan[:], T.i4[:], tau, BASE, Alu.is_gt, Alu.mult), ["i4", "cf"], ["kscan"])
@@ -239,24 +238,29 @@ def rank_program(g, core, T, topo):
         else:
             V(ts(out, in_, 0.015625, None, Alu.mult), [name], [key])
 
-    def addresses(c, sc, keys, a, z, pa, sums):
-        P(mm(T[pa][:, 0:z - a], T.uq[:], T.usq[:], c[:, a:z], sc[:, a:z], True, True), keys + ["uq"], [pa])
-        mine = ["bits%d" % h for h in range(a // H, z // H)]
-        V(ts(T.wk[:, a:z], T[pa][:, 0:z - a], 0.0, pw, Alu.is_gt, Alu.mult), [pa, "pw"], mine)
-        if sums:
-            V(qz(T.aq[:, 0:128], T.aqs[:, 0:128], T.wk[:, 0:512]), ["bits0", "bits1"] + fls[:4], ["bitq", "flq0"])
-        for j, name in sums:
+    def bits(c, sc, keys, a, z, pa):
+        P(mm(T[pa][:, 0:z - a], T.uq[:], T.usq[:], c, sc, True, True), keys + ["uq"], [pa])
+        V(ts(T.wk[:, a:z], T[pa][:, 0:z - a], 0.0, pw, Alu.is_gt, Alu.mult), [pa, "pw"], ["bits%d" % h for h in range(a // H, z // H)])
+
+    def sums(*which):
+        V(qz(T.aq[:, 0:128], T.aqs[:, 0:128], T.wk[:, 0:512]), ["bits0", "bits1"] + fls[:4], ["bitq", "flq0"])
+        for j in which:
+            name = ("po", "pc")[j]
             P(mm(T[name][:, 0:128], *kside(j), *work(0), True, True), ["kq%d" % j, "bitq", "flq0"], [name])
 
-    def send_addresses(t, a, z, pc):
-        name, h = "rs%d" % t, a // H
-        V(scan(T.v1[:, a // 4:z // 4], T[pc][:, a // 4:z // 4], (z - a) // 4), ["kscan", pc], ["v1%d" % h])
-        V(ts(T[name][:, a // 16:z // 16], T.v1[:, a // 4 + 3:z // 4:4], scol4, None, Alu.mult), ["v1%d" % h, "scol4"], [name + str(h)])
-        hop(T["ra%d" % t][:, a // 16:z // 16], T[name][:, a // 16:z // 16], "ar%d%d" % (t, h), nxt, [name + str(h)])
+    def send_addresses(t):
+        name = "rs%d" % t
+        V(scan(T.v1[:], T.pc[:, 0:64], 64), ["kscan", "pc"], ["v1"])
+        V(ts(T[name][:], T.v1[:, 3:64:4], scol4, None, Alu.mult), ["v1", "scol4"], [name])
+        hop(T["ra%d" % t][:], T[name][:], "ar%d" % t, nxt, [name])
 
-    def slots(t):
+    def owns():
         S(act(T.own0[:], T.po[:, 0:64], bias=ge), ["po", "ge"], ["own0"])
         S(act(T.own[:], T.po[:, 0:64]), ["po"], ["own"])
+
+    def slots(t):
+        if t:
+            owns()
         for j in range(SHIFTS):
             a = C + 256 * (j // 4)
             o = "own" if j else "own0"
@@ -273,7 +277,6 @@ def rank_program(g, core, T, topo):
             hop(T["oa%d" % t][:], T[name][:], "ao%d" % t, nxt, [name + "a", name + "b"])
 
     for t in range(VISITS):
-        sc_, ss_ = (T["l%dc" % t], T["l%ds" % t]) if t else (T.aq[:, 192:192 + C], T.aqs[:, 192:192 + C])
         yc, ys = T["y%dc" % t], T["y%ds" % t]
         final = t + 1 == VISITS
         lo = 4 * M + 4 * C * t
@@ -283,63 +286,39 @@ def rank_program(g, core, T, topo):
         land = T["l%dc" % (t + 1)]
 
         if t == 0:
-            P(mm(T.pa[:, 0:C], T.uq[:], T.usq[:], sc_, ss_, True, True), ["state0", "uq"], ["pa"])
-            V(ts(T.wk[:, 0:C], T.pa[:, 0:C], 0.0, pw, Alu.is_gt, Alu.mult), ["pa", "pw"], ["bits0", "bits1"])
-            V(qz(T.aq[:, 0:128], T.aqs[:, 0:128], T.wk[:, 0:512]), ["bits0", "bits1"] + fls[:4], ["bitq", "flq0"])
-            for j, name in ((0, "po"), (1, "pc")):
-                P(mm(T[name][:, 0:128], *kside(j), *work(0), True, True), ["kq%d" % j, "bitq", "flq0"], [name])
+            bits(T.aq[:, 192:192 + C], T.aqs[:, 192:192 + C], ["state0"], 0, C, "pa")
+            sums(0, 1)
             V(ts(T.off[:], T.po[:, 0:64], bcol, None, Alu.add), ["po", "cf"], ["off0", "off1"])
-            gather("s", T.bt[:, 16 * GV0:4 * C], T.pool[:, 0:lo], T.off[:, GV0:64], pk + ["off0", "off1"], "bts0")
-            gather("v", T.bt[:, 0:16 * GV0], T.pool[:, 0:lo], T.off[:, 0:GV0], pk + ["off0", "off1"], "btv0")
-            V(qz(T.bq[:], T.bs[:], T.bt[:]), ["bts0", "btv0", "bts1", "btv1"], ["bq0", "bq1"])
-            for b in range(4):
-                name = SETS[0][b]
-                calls = [(mm(T[name][:, 0:C], *wside(b), sc_, ss_, b < 2, b > 1), ["state0", "w%d" % b, "ws"]),
-                         (mm(T[name][:, 0:C], *eside(b), T.bq[:], T.bs[:], b > 1, b < 2), ["bq0", "bq1", "eq%d" % b])]
-                for fn, keys in (calls if b < 2 else calls[::-1]):
-                    P(fn, keys, [name])
-                scaled(COPY[0][0][b], T.yt[:, b:4 * C:4], T[name][:, 0:C], name, "yt0%d" % b)
-            V(qz(yc[:], ys[:], T.yt[:]), ["yt%d%d" % (h, b) for h in range(2) for b in range(4)], yq)
-            slots(0)
-        else:
-            parts = PARTS[t - 1]
-            for h in range(2):
-                a, z, gv = H * h, H * h + H, GV[t][h]
-                gather(LOOK[t][h], T.look[:, a:z], T.tab[:, 0:M], T["ra%d" % t][:, 8 * h:8 * h + 8], ["tab", "tabb"], "look%d" % h,
-                       after=[("ar%d%d" % (t, h if parts > 1 else 0), before)])
+            owns()
+        for h in range(2):
+            a, z, gv = H * h, H * h + H, GV[t][h]
+            if t:
+                gather(LOOK[t][h], T.look[:, a:z], T.tab[:, 0:M], T["ra%d" % t][:, 8 * h:8 * h + 8], ["tab", "tabb"], "look%d" % h, after=[("ar%d" % t, before)])
                 V(scan(T.scan[:, a:z], T.look[:, a:z], H), ["kscan", "look%d" % h], ["scan%d" % h])
                 V(ts(T.off[:, 32 * h:32 * h + 32], T.scan[:, a + 3:z:4], scol, bcol, Alu.mult, Alu.add), ["scan%d" % h, "scol", "cf"], ["off%d" % h])
-                gather("s", T.bt[:, 4 * a + 16 * gv:4 * z], T.pool[:, 0:lo], T.off[:, 32 * h + gv:32 * h + 32], pk + ["off%d" % h], "bts%d" % h)
-                if gv:
-                    gather("v", T.bt[:, 4 * a:4 * a + 16 * gv], T.pool[:, 0:lo], T.off[:, 32 * h:32 * h + gv], pk + ["off%d" % h], "btv%d" % h)
-                V(qz(T.bq[:, a:z], T.bs[:, a:z], T.bt[:, 4 * a:4 * z]), ["bts%d" % h, "btv%d" % h], ["bq%d" % h])
-                for b in range(4):
-                    name = SETS[h][b]
-                    P(mm(T[name][:, 0:H], *wside(b), sc_[:, a:z], ss_[:, a:z], True, False), ["w%d" % b, "ws"], [name],
+            gather("s", T.bt[:, 4 * a + 16 * gv:4 * z], T.pool[:, 0:lo], T.off[:, 32 * h + gv:32 * h + 32], pk + ["off%d" % h], "bts%d" % h)
+            gather("v", T.bt[:, 4 * a:4 * a + 16 * gv], T.pool[:, 0:lo], T.off[:, 32 * h:32 * h + gv], pk + ["off%d" % h], "btv%d" % h)
+            V(qz(T.bq[:, a:z], T.bs[:, a:z], T.bt[:, 4 * a:4 * z]), ["bts%d" % h, "btv%d" % h], ["bq%d" % h])
+            for b in range(4):
+                name = (SETS[0], BANKS[t])[h][b]
+                if t:
+                    P(mm(T[name][:, 0:H], *wside(b), T["l%dc" % t][:, a:z], T["l%ds" % t][:, a:z], True, False), ["w%d" % b, "ws"], [name],
                       after=[("arr%d" % t, before), ("arc%d%d" % (t, h), before)])
-                    P(mm(T[name][:, 0:H], *eside(b), T.bq[:, a:z], T.bs[:, a:z], False, True), ["bq%d" % h, "eq%d" % b], [name])
-                    scaled(COPY[t][h][b], T.yt[:, 4 * a + b:4 * z:4], T[name][:, 0:H], name, "yt%d%d" % (h, b))
-                V(qz(yc[:, a:z], ys[:, a:z], T.yt[:, 4 * a:4 * z]), ["yt%d%d" % (h, b) for b in range(4)], [yq[h]])
+                else:
+                    P(mm(T[name][:, 0:H], *wside(b), T.aq[:, 192 + a:192 + z], T.aqs[:, 192 + a:192 + z], True, False), ["state0", "w%d" % b, "ws"], [name])
+                P(mm(T[name][:, 0:H], *eside(b), T.bq[:, a:z], T.bs[:, a:z], False, True), ["bq%d" % h, "eq%d" % b], [name])
+                scaled(COPY[t][h][b], T.yt[:, 4 * a + b:4 * z:4], T[name][:, 0:H], name, "yt%d%d" % (h, b))
+            V(qz(yc[:, a:z], ys[:, a:z], T.yt[:, 4 * a:4 * z]), ["yt%d%d" % (h, b) for b in range(4)], [yq[h]])
+        if t == 0:
+            slots(0)
         for h in range(2):
             hop(words(land, H * h, H * h + H), words(yc, H * h, H * h + H), "arc%d%d" % (t + 1, h), dst, [yq[h]])
-        if final and YSPLIT:
-            for h in range(2):
-                hop(T.fins[:, H * h:H * h + H], ys[:, H * h:H * h + H], "arr3" + "ab"[h], dst, [yq[h]])
-        else:
-            hop(T.fins[:, 0:C] if final else T["l%ds" % (t + 1)][:], ys[:], "arr%d" % (t + 1), dst, yq)
+        hop(T.fins[:, 0:C] if final else T["l%ds" % (t + 1)][:], ys[:], "arr%d" % (t + 1), dst, yq)
         if not final:
-            if PARTS[t] == 1 and ASPLIT[t]:
-                addresses(yc, ys, yq[:1], 0, H, "pr0", ())
-                addresses(yc, ys, yq[1:], H, C, "pa", ((1, "pc"), (0, "po")))
-                send_addresses(t + 1, 0, C, "pc")
-            elif PARTS[t] == 1:
-                addresses(yc, ys, yq, 0, C, "pa", ((1, "pc"), (0, "po")))
-                send_addresses(t + 1, 0, C, "pc")
-            else:
-                addresses(yc, ys, yq[:1], 0, H, "pr0", ((1, "pr1"),))
-                send_addresses(t + 1, 0, H, "pr1")
-                addresses(yc, ys, yq[1:], H, C, "pa", ((1, "pc"), (0, "po")))
-                send_addresses(t + 1, H, C, "pc")
+            bits(yc[:, 0:H], ys[:, 0:H], yq[:1], 0, H, ABANK[t])
+            bits(yc[:, H:C], ys[:, H:C], yq[1:], H, C, "pa")
+            sums(1, 0)
+            send_addresses(t + 1)
         for h, (a, z) in enumerate(((0, H), (H, C)) if len(WRITE[t]) == 8 else ((0, C),)):
             for b in range(4):
                 name = SETS[h if final else 0][(b + 2) % 4]
@@ -357,27 +336,22 @@ def rank_program(g, core, T, topo):
         V(scan(T.mscan[:, 4 * a:4 * z], T.tab[:, 4 * a:4 * z], 4 * (z - a)), ["kscan", "tab", "tabb"], ["mscan" + key])
         V(ts(T.moff[:, a:z], T.mscan[:, 4 * a + 3:4 * z:4], scol, bcol, Alu.mult, Alu.add), ["mscan" + key, "scol", "cf"], ["moff" + key])
         gather("s", T.mc[:, 16 * a:16 * (a + share)], T.pool[:], T.moff[:, a:a + share], pk + ["moff" + key], "ms" + key)
-        if a + share < z:
-            gather("v", T.mc[:, 16 * (a + share):16 * z], T.pool[:], T.moff[:, a + share:z], pk + ["moff" + key], "mv" + key)
+        gather("v", T.mc[:, 16 * (a + share):16 * z], T.pool[:], T.moff[:, a + share:z], pk + ["moff" + key], "mv" + key)
         V(qz(T.qmc[:, 4 * a:4 * z], T.fins[:, C + 4 * a:C + 4 * z], T.mc[:, 16 * a:16 * z]), ["ms" + key, "mv" + key], ["qm" + key])
 
-    codes = [("arc30", home), ("arc31", home)]
-    planes = [("arr3a", home), ("arr3b", home)] if YSPLIT else [("arr3", home)]
+    codes, plane = [("arc30", home), ("arc31", home)], [("arr3", home)]
     qm = ["qm%d" % a for a, z, share in LAST]
-    for h, (a, z) in enumerate(((0, H), (H, C)) if YSPLIT else ((0, C),)):
-        name = YBANK[h]
-        P(mm(T[name][:, 0:z - a], *wside(0), T.l3c[:, a:z], T.fins[:, a:z], True, True), ["w0", "ws"], [name],
-          after=[codes[h], planes[h]] if YSPLIT else codes + planes)
-        if YCOPY[h] == "s":
-            S(act(T.ysb[:, a:z], T[name][:, 0:z - a]), [name], ["ysb%d" % h])
-        else:
-            V(lambda a=a, z=z, name=name: v.tensor_copy(T.ysb[:, a:z], T[name][:, 0:z - a]), [name], ["ysb%d" % h])
-        load(YQ[h], T.y[:, a:z], T.ysb[:, a:z], ["ysb%d" % h], (), "dy%d" % h)
-    load(OQ[0], T.oc[:, 0:4 * C], T.l3c[:].bitcast(dt.uint8), (), (), "dsc", after=codes)
+    P(mm(T.pr0[:, 0:C], *wside(0), T.l3c[:], T.fins[:, 0:C], True, True), ["w0", "ws"], ["pr0"], after=codes + plane)
+    if YCOPY == "s":
+        S(act(T.ysb[:], T.pr0[:, 0:C]), ["pr0"], ["ysb"])
+    else:
+        V(lambda: v.tensor_copy(T.ysb[:], T.pr0[:, 0:C]), ["pr0"], ["ysb"])
+    load(YQ, T.y[:], T.ysb[:], ["ysb"], (), "dy")
+    load(OQ[0], T.oc[:, 0:4 * C], words(T.l3c, 0, C), (), (), "dsc", after=codes)
     for h, (a, z) in enumerate(STORES):
         load(OQ[1 + h], T.oc[:, 4 * C + 16 * a:4 * C + 16 * z], words(T.qmc, 4 * a, 4 * z), ["qm%d" % a2 for a2, z2, share in LAST if a <= a2 < z], (), "dm%d" % h)
     for k in range(4):
-        load(SQ[k], T.osc[4 * k:4 * k + 4, :], T.fins[32 * k:32 * k + 4, :], qm, (), "ds%d" % k, after=planes)
+        load(SQ[k], T.osc[4 * k:4 * k + 4, :], T.fins[32 * k:32 * k + 4, :], qm, (), "ds%d" % k, after=plane)
 
     order = ORDER or list(range(len(ops)))
     place = {d: i for i, d in enumerate(order)}

@@ -6,30 +6,30 @@ BIG, BASE = 16384.0, 4194304.0
 SHIFTS = 8
 H = C // 2
 EW = 514
-GV = {0: (12, 10), 1: (12, 10), 2: (12, 10)}
-LOOK = {1: "vs", 2: "vs"}
+GV = {0: (14, 12), 1: (14, 14), 2: (14, 12)}
+LOOK = {1: "ss", 2: "ss"}
 COPY = {0: ('sssv', 'sssv'), 1: ('sssv', 'svsv'), 2: ('ssss', 'ssss')}
 WRITE = {0: 'ssss', 1: 'ssss', 2: 'ssssssss'}
 BANKS = {0: ("pa", "po", "pr0", "pr1"), 1: ("pa", "po", "pc", "ps"), 2: ("pa", "po", "pc", "ps")}
 ABANK = {0: "pr2", 1: "pr0"}
 WA = 2
-LAST = ((0, 64, 38), (64, 128, 36))
+LAST = ((0, 64, 36), (64, 128, 32))
 STORES = ((0, 64), (64, 128))
 YCOPY = 's'
 YQ = 's'
 OQ = 'yyyyy'
 SQ = 'yyys'
-ORDER = [0, 1, 6, 10, 2, 3, 9, 4, 5, 23, 17, 25, 21, 8, 22, 24, 7, 18, 26, 28, 34, 30, 36, 31, 37, 32, 15, 12, 41, 55, 35, 14, 38, 33, 40, 11, 39, 16, 27, 56, 13,
-         52, 42, 57, 19, 29, 20, 58, 51, 50, 59, 70, 53, 76, 61, 73, 48, 60, 64, 67, 65, 83, 49, 62, 63, 80, 66, 86, 54, 102, 68, 81, 71, 74, 69, 103, 77, 101,
-         72, 98, 75, 89, 82, 92, 97, 99, 90, 100, 84, 96, 78, 93, 91, 104, 87, 85, 79, 88, 105, 94, 43, 106, 111, 107, 95, 45, 114, 108, 44, 116, 115, 109, 117,
-         124, 110, 130, 118, 125, 132, 119, 131, 128, 133, 121, 120, 126, 134, 141, 122, 140, 135, 46, 123, 143, 129, 136, 142, 127, 137, 145, 47, 113, 147,
-         149, 138, 146, 139, 112, 148, 158, 177, 144, 159, 150, 160, 178, 161, 162, 170, 151, 152, 179, 153, 164, 180, 167, 154, 163, 173, 156, 155, 192, 181,
-         171, 157, 168, 174, 182, 165, 169, 183, 175, 172, 189, 166, 186, 187, 176, 190, 193, 188, 184, 191, 196, 199, 194, 185, 195, 200, 201, 197, 217, 202,
-         203, 218, 205, 204, 219, 213, 226, 206, 211, 228, 214, 233, 209, 207, 220, 225, 215, 208, 229, 210, 234, 227, 230, 216, 232, 231, 221, 198, 235, 222,
-         236, 237, 223, 238, 239, 224, 240, 241, 243, 262, 242, 212, 263, 244, 264, 245, 265, 266, 271, 268, 247, 249, 258, 246, 274, 252, 267, 277, 269, 275,
-         300, 278, 270, 248, 272, 276, 301, 279, 259, 273, 250, 302, 253, 260, 280, 255, 251, 256, 303, 254, 282, 298, 257, 296, 304, 294, 261, 295, 305, 299,
-         281, 286, 297, 284, 306, 290, 288, 285, 307, 292, 289, 283, 313, 293, 287, 291, 314, 308, 315, 309, 316, 310, 311, 321, 317, 312, 323, 318, 322, 325,
-         326, 324, 319, 327, 320]
+ORDER = [0, 1, 6, 10, 2, 3, 9, 4, 5, 21, 23, 17, 25, 8, 24, 22, 11, 16, 26, 7, 31, 34, 28, 35, 30, 18, 55, 33, 38, 41, 14, 32, 15, 39, 12, 27, 56, 20, 57, 36, 13,
+         37, 29, 42, 40, 58, 19, 51, 52, 50, 59, 67, 70, 76, 61, 48, 60, 73, 64, 65, 81, 62, 63, 80, 66, 86, 49, 68, 97, 71, 99, 82, 74, 69, 77, 98, 72, 83, 102,
+         96, 75, 87, 100, 101, 89, 103, 92, 53, 90, 78, 88, 84, 93, 104, 91, 79, 85, 94, 105, 44, 106, 54, 107, 111, 114, 43, 95, 108, 45, 115, 116, 110, 109,
+         117, 132, 118, 133, 119, 120, 128, 121, 124, 134, 141, 130, 140, 122, 126, 146, 143, 135, 123, 127, 148, 149, 113, 145, 136, 46, 112, 147, 144, 129,
+         142, 137, 131, 150, 138, 125, 151, 47, 152, 139, 153, 167, 154, 158, 173, 156, 177, 155, 159, 157, 192, 178, 189, 164, 160, 170, 183, 179, 186, 161,
+         162, 181, 180, 163, 165, 182, 174, 168, 217, 171, 166, 175, 193, 169, 184, 218, 187, 172, 190, 194, 185, 188, 191, 219, 176, 195, 220, 199, 201, 197,
+         200, 198, 202, 221, 203, 222, 204, 205, 215, 206, 209, 223, 226, 213, 216, 207, 211, 232, 234, 225, 228, 214, 208, 230, 233, 229, 196, 212, 231, 227,
+         235, 224, 236, 237, 238, 274, 271, 262, 268, 239, 243, 240, 241, 210, 263, 244, 258, 242, 264, 255, 277, 245, 252, 265, 266, 247, 246, 267, 300, 269,
+         272, 301, 275, 278, 270, 248, 249, 276, 302, 273, 256, 279, 250, 253, 303, 259, 257, 280, 254, 304, 260, 251, 282, 298, 294, 296, 305, 261, 297, 306,
+         299, 284, 281, 290, 288, 283, 307, 292, 285, 286, 295, 291, 313, 289, 287, 308, 293, 314, 309, 315, 316, 321, 311, 310, 318, 317, 319, 312, 323, 322,
+         327, 326, 320, 324, 325]
 
 
 def _sb(n, d):

from concourse.mybir import dt, AluOpType as Alu, AxisListType, ActivationFunctionType as Act

C, M, VISITS = 256, 512, 3
X4, U8, BF, F32, U16, I32 = "float8_e4m3fn_x4", "uint8", "bfloat16", "float32", "uint16", "int32"
BIG, BASE = 16384.0, 4194304.0
SHIFTS = 8
H = C // 2
EW = 514
GV = {0: (14, 12), 1: (14, 14), 2: (14, 12)}
LOOK = {1: "ss", 2: "ss"}
COPY = {0: ('sssv', 'sssv'), 1: ('sssv', 'svsv'), 2: ('ssss', 'ssss')}
WRITE = {0: 'ssss', 1: 'ssss', 2: 'ssssssss'}
BANKS = {0: ("pa", "po", "pr0", "pr1"), 1: ("pa", "po", "pc", "ps"), 2: ("pa", "po", "pc", "ps")}
ABANK = {0: "pr2", 1: "pr0"}
WA = 2
LAST = ((0, 64, 36), (64, 128, 32))
STORES = ((0, 64), (64, 128))
YCOPY = 's'
YQ = 's'
OQ = 'yyyyy'
SQ = 'yyys'
ORDER = [0, 1, 6, 10, 2, 3, 9, 4, 5, 21, 23, 17, 25, 8, 24, 22, 11, 16, 26, 7, 31, 34, 28, 35, 30, 18, 55, 33, 38, 41, 14, 32, 15, 39, 12, 27, 56, 20, 57, 36, 13,
         37, 29, 42, 40, 58, 19, 51, 52, 50, 59, 67, 70, 76, 61, 48, 60, 73, 64, 65, 81, 62, 63, 80, 66, 86, 49, 68, 97, 71, 99, 82, 74, 69, 77, 98, 72, 83, 102,
         96, 75, 87, 100, 101, 89, 103, 92, 53, 90, 78, 88, 84, 93, 104, 91, 79, 85, 94, 105, 44, 106, 54, 107, 111, 114, 43, 95, 108, 45, 115, 116, 110, 109,
         117, 132, 118, 133, 119, 120, 128, 121, 124, 134, 141, 130, 140, 122, 126, 146, 143, 135, 123, 127, 148, 149, 113, 145, 136, 46, 112, 147, 144, 129,
         142, 137, 131, 150, 138, 125, 151, 47, 152, 139, 153, 167, 154, 158, 173, 156, 177, 155, 159, 157, 192, 178, 189, 164, 160, 170, 183, 179, 186, 161,
         162, 181, 180, 163, 165, 182, 174, 168, 217, 171, 166, 175, 193, 169, 184, 218, 187, 172, 190, 194, 185, 188, 191, 219, 176, 195, 220, 199, 201, 197,
         200, 198, 202, 221, 203, 222, 204, 205, 215, 206, 209, 223, 226, 213, 216, 207, 211, 232, 234, 225, 228, 214, 208, 230, 233, 229, 196, 212, 231, 227,
         235, 224, 236, 237, 238, 274, 271, 262, 268, 239, 243, 240, 241, 210, 263, 244, 258, 242, 264, 255, 277, 245, 252, 265, 266, 247, 246, 267, 300, 269,
         272, 301, 275, 278, 270, 248, 249, 276, 302, 273, 256, 279, 250, 253, 303, 259, 257, 280, 254, 304, 260, 251, 282, 298, 294, 296, 305, 261, 297, 306,
         299, 284, 281, 290, 288, 283, 307, 292, 285, 286, 295, 291, 313, 289, 287, 308, 293, 314, 309, 315, 316, 321, 311, 310, 318, 317, 319, 312, 323, 322,
         327, 326, 320, 324, 325]


def _sb(n, d):
    return ("sbuf", [128, n], d)


SCRATCH = {
    "xt": _sb(4 * C, BF), "ut": _sb(512, BF), "pool": _sb(4 * M + VISITS * 4 * C, BF),
    "wq": _sb(512, X4), "wsq": _sb(512, U8), "uq": _sb(128, X4), "usq": _sb(128, U8),
    "aq": _sb(192 + C, X4), "aqs": _sb(192 + C, U8), "wk": _sb(768, BF),
    "l1c": _sb(C, X4), "l1s": _sb(C, U8), "l2c": _sb(C, X4), "l2s": _sb(C, U8),
    "l3c": _sb(C, X4), "fins": _sb(C + M, U8), "qmc": _sb(M, X4),
    "y0c": _sb(C, X4), "y0s": _sb(C, U8), "y1c": _sb(C, X4), "y1s": _sb(C, U8), "y2c": _sb(C, X4), "y2s": _sb(C, U8),
    "off": _sb(64, U16), "own": _sb(64, F32), "own0": _sb(64, F32), "bt": _sb(4 * C, BF), "bq": _sb(C, X4), "bs": _sb(C, U8), "yt": _sb(4 * C, BF),
    "v1": _sb(64, F32), "v2": _sb(64, F32),
    "rs1": _sb(16, U16), "rs2": _sb(16, U16), "ra1": _sb(16, U16), "ra2": _sb(16, U16),
    "oa0": _sb(16, U16), "os1": _sb(16, U16), "os2": _sb(16, U16), "oa1": _sb(16, U16), "oa2": _sb(16, U16),
    "tab": _sb(M + 256, F32), "val": _sb(VISITS * C, F32), "scan": _sb(C, F32), "mscan": _sb(M, F32), "moff": _sb(128, U16),
    "mc": _sb(4 * M, BF), "look": _sb(C, F32), "seq": _sb(C, F32),
    "c64": _sb(EW, BF), "ident": _sb(128, BF), "et": _sb(1026, BF), "eq": _sb(512, X4), "es": _sb(512, U8),
    "kt": _sb(1536, BF), "kq": _sb(384, X4), "ks": _sb(384, U8),
    "iq": _sb(1, I32), "ci": _sb(8, I32), "cf": _sb(8, F32), "col": _sb(8, F32), "i18": _sb(18, F32), "t18": _sb(18, F32),
    "ia": _sb(512, BF), "gm": _sb(32, BF), "ic": _sb(128, BF), "i4": _sb(C, BF), "t4": _sb(4, F32),
    "spare": _sb(2, F32), "kscan": _sb(C, BF), "ysb": _sb(C, F32),
    "pa": ("psum", [128, 512], F32), "po": ("psum", [128, 512], F32), "pc": ("psum", [128, 512], F32), "ps": ("psum", [128, 512], F32),
    "pr0": ("psum", [128, 512], F32), "pr1": ("psum", [128, 512], F32), "pr2": ("psum", [128, 512], F32), "pr3": ("psum", [128, 512], F32),
}
DMAS = ["dx", "du", "dm", "dws", "dwa", "dwb", "dy", "dsc", "dm0", "dm1", "dm2", "dm3", "ds0", "ds1", "ds2", "ds3"]
SEMAPHORES = ["qv", "qs", "qt", "qg", "arr1", "arr2", "arr3", "ar1", "ar2", "ao1", "ao2",
              "arc10", "arc11", "arc20", "arc21", "arc30", "arc31", "sent"] + DMAS
PSUM = ("pa", "po", "pc", "ps", "pr0", "pr1", "pr2", "pr3")
SETS = (("pr0", "pr1", "pr2", "pr3"), ("pa", "po", "pc", "ps"))


def rank_program(g, core, T, topo):
    rank = T.rank_of(core)
    if rank is None:
        return
    n = len(T.cores)
    eng = {"v": g.vector, "s": g.scalar, "t": g.tensor, "g": g, "y": g.sync}
    counter = {"v": "qv", "s": "qs", "t": "qt", "g": "qg"}
    ops, writer, readers, bank = [], {}, {}, {}

    def op(q, fn, reads=(), writes=(), dma=None, after=()):
        me = len(ops)
        deps, behind = set(), set()
        for k in reads:
            if k not in PSUM and k in writer:
                deps.add(writer[k])
        for k in writes:
            if k in PSUM:
                continue
            for d in [writer.get(k)] + readers.get(k, []):
                if d is not None:
                    deps.add(d)
        for k in list(reads) + list(writes):
            if k in PSUM:
                for d in bank.setdefault(k, []):
                    if ops[d]["q"] != q:
                        deps.add(d)
                    elif q == "t":
                        behind.add(d)
                bank[k].append(me)
        for k in reads:
            readers.setdefault(k, []).append(me)
        for k in writes:
            writer[k] = me
            readers[k] = []
        ops.append({"q": q, "fn": fn, "deps": deps, "behind": behind, "dma": dma, "after": list(after), "need": False})

    def V(fn, r=(), w=(), **k):
        op("v", fn, r, w, **k)

    def S(fn, r=(), w=(), **k):
        op("s", fn, r, w, **k)

    def P(fn, r=(), w=(), **k):
        op("t", fn, r, w, **k)

    def G(fn, r=(), w=(), **k):
        op("g", fn, r, w, **k)

    v, s, pe = g.vector, g.scalar, g.tensor

    def ts(out, in0, a, b, o0, o1=None):
        if o1 is None:
            return lambda: v.tensor_scalar(out, in0, a, None, o0)
        return lambda: v.tensor_scalar(out, in0, a, b, o0, o1)

    def mm(out, w, ws, x, xs, start, stop):
        return lambda: pe.matmul_mx(out, w, ws, x, xs, start, stop)

    def qz(c, sc, t):
        return lambda: v.quantize_mx(c, sc, t)

    def scan(out, data, width):
        return lambda: v.tensor_tensor_scan(out, T.kscan[:, 0:width], data, 0.0, Alu.mult, Alu.add)

    def iota(out, pattern, base, cm, small=True):
        if small:
            return lambda: g.iota(out, pattern, base, cm, allow_small_or_imprecise_dtypes=True)
        return lambda: g.iota(out, pattern, base, cm)

    def act(out, in_, scale=None, bias=None):
        if bias is not None:
            return lambda: s.activation(out, in_, Act.Identity, bias=bias)
        if scale is None:
            return lambda: s.activation(out, in_, Act.Copy)
        return lambda: s.activation(out, in_, Act.Copy, scale=scale)

    def load(q, out, in_, reads, writes, sem, after=()):
        op(q, lambda: eng[q].dma_start(out, in_), reads, writes, dma=sem, after=after)

    load("y", T.xt[:], T.x[:], (), ["xt"], "dx")
    load("s", T.ut[:], T.u[:], (), ["ut"], "du")
    load("y", T.pool[:, 0:4 * M], T.m[:], (), ["pool_m"], "dm")
    load("y", T.wsq[:], T.ws[:], (), ["ws"], "dws")
    load("y", T.wq[:, 0:128 * WA].bitcast(dt.uint8), T.wc[:, 0:512 * WA], (), ["w%d" % b for b in range(WA)], "dwa")
    load("y", T.wq[:, 128 * WA:512].bitcast(dt.uint8), T.wc[:, 512 * WA:2048], (), ["w%d" % b for b in range(WA, 4)], "dwb")

    fls = ["fl%d" % j for j in range(SHIFTS)]
    G(iota(T.iq[:], [[0, 1]], 0, 1, False), (), ["iq"])
    G(iota(T.ia[:], [[1, 32], [0, 4], [-1, 4]], 0, 0), (), ["ia"])
    G(iota(T.i18[:], [[1, 18]], -2, 0), (), ["i18"])
    G(iota(T.ic[:], [[4, 8], [0, 4], [1, 4]], 0, 0), (), ["ic"])
    V(lambda: v.memset(T.c64[:], 64.0), (), ["c64"])
    G(lambda: g.affine_select(T.ident[:], T.c64[:, 0:128], [[-1, 128]], Alu.is_equal, 0.0, 0, 1), ["c64"], ["ident"])
    G(iota(T.i4[:], [[0, C // 4], [1, 4]], 0, 0), (), ["i4"])
    G(iota(T.seq[:], [[4, C]], 0, 0), (), ["seq"])
    G(iota(T.spare[:], [[128, 2]], M, 1), (), ["spare"])
    S(act(T.et[:, 0:EW], T.c64[:], 0.0), ["c64"], ["et0"])
    S(act(T.et[:, EW:1026], T.c64[:, 0:512], 0.0), ["c64"], ["et1"])
    S(act(T.kt[:, 512:1024], T.c64[:, 0:512], 0.0), ["c64"], ["kc%d" % t for t in range(4)])
    S(act(T.wk[:, C:768], T.c64[:, 0:512], 0.0), ["c64"], fls)
    for h in range(2):
        S(act(T.et[:, 513 * h + 2:513 * h + 512:4], T.ident[:]), ["ident"], ["et%d" % h])
    V(ts(T.ci[:, 1:2], T.iq[:], 2, 28, Alu.logical_shift_right, Alu.bitwise_and), ["iq"], ["ci1"])
    V(ts(T.ci[:, 4:5], T.iq[:], 15, None, Alu.bitwise_and), ["iq"], ["ci4"])
    V(ts(T.ci[:, 0:1], T.iq[:], 2, None, Alu.logical_shift_right), ["iq"], ["ci0"])
    V(ts(T.ci[:, 2:3], T.iq[:], 2, 3, Alu.logical_shift_right, Alu.bitwise_and), ["iq"], ["ci2"])
    V(ts(T.ci[:, 3:4], T.iq[:], 3, None, Alu.bitwise_and), ["iq"], ["ci3"])
    V(lambda: v.tensor_copy(T.cf[:, 0:5], T.ci[:, 0:5]), ["ci0", "ci1", "ci2", "ci3", "ci4"], ["cf"])
    q4, g4, tau, bcol, icol = [T.cf[:, j:j + 1] for j in range(5)]
    p2, pw, ge, scol, scol4 = [T.col[:, j:j + 1] for j in range(5)]
    V(ts(T.kt[:, 0:512], T.ia[:], g4, None, Alu.is_equal), ["ia", "cf"], ["ka"])
    V(ts(T.t18[:], T.i18[:], icol, 1.0, Alu.is_lt, Alu.add), ["i18", "cf"], ["t18"])
    V(qz(T.kq[:, 0:128], T.ks[:, 0:128], T.kt[:, 0:512]), ["ka"], ["kq0"])
    V(lambda: v.tensor_reduce(p2, T.t18[:], AxisListType.X, Alu.mult), ["t18"], ["p2"])
    V(ts(T.kt[:, 1024:1536:4], T.ic[:], q4, BIG, Alu.is_equal, Alu.mult), ["ic", "cf"], ["kd0"])
    V(ts(pw, icol, 9.0, p2, Alu.is_lt, Alu.mult), ["cf", "p2"], ["pw"])
    V(qz(T.uq[:], T.usq[:], T.ut[:]), ["ut"], ["uq"])
    V(ts(T.gm[:], T.ic[:, 0:128:4], g4, None, Alu.is_equal), ["ic", "cf"], ["gm"])
    for t in range(4):
        S(act(T.kt[:, 512 + 5 * t:1024:16], T.gm[:]), ["gm"], ["kc%d" % t])
    V(ts(ge, bcol, tau, BIG, Alu.is_ge, Alu.mult), ["cf"], ["ge"])
    for t in range(1, 4):
        S(act(T.kt[:, 1024 + t:1536:4], T.kt[:, 1024:1536:4]), ["kd0"], ["kd%d" % t])
    S(act(T.tab[:, 0:C], T.seq[:]), ["seq"], ["tab"])
    S(act(T.tab[:, C:M], T.seq[:], bias=float(4 * C)), ["seq"], ["tabb"])
    for t in range(VISITS):
        S(act(T.val[:, C * t:C * t + C], T.seq[:], bias=float(4 * M + 4 * C * t)), ["seq"], ["val%d" % t])
    for h in range(2):
        V(qz(T.eq[:, 256 * h:256 * h + 256], T.es[:, 256 * h:256 * h + 256], T.et[:, 2 - 2 * h:1026 - 2 * h]), ["et0", "et1"], ["eq%d" % (2 * h), "eq%d" % (2 * h + 1)])
    V(qz(T.kq[:, 128:384], T.ks[:, 128:384], T.kt[:, 512:1536]), ["kc%d" % t for t in range(4)] + ["kd%d" % t for t in range(4)], ["kq1"])
    V(ts(T.t4[:], T.i4[:, 0:4], tau, 1.0 / BASE, Alu.is_le, Alu.max), ["i4", "cf"], ["t4"])
    V(ts(T.kscan[:], T.i4[:], tau, BASE, Alu.is_gt, Alu.mult), ["i4", "cf"], ["kscan"])
    V(lambda: v.tensor_reduce(scol, T.t4[:], AxisListType.X, Alu.mult), ["t4"], ["scol"])
    V(ts(scol4, scol, 0.25, None, Alu.mult), ["scol"], ["scol4"])
    V(qz(T.aq[:, 192:192 + C], T.aqs[:, 192:192 + C], T.xt[:]), ["xt"], ["state0"])

    engines = [0]

    def kside(j):
        return T.kq[:, 128 * j:128 * j + 128], T.ks[:, 128 * j:128 * j + 128]

    def wside(b):
        return T.wq[:, 128 * b:128 * b + 128], T.wsq[:, 128 * b:128 * b + 128]

    def eside(b):
        return T.eq[:, 128 * b:128 * b + 128], T.es[:, 128 * b:128 * b + 128]

    def work(a):
        return T.aq[:, a:a + 128], T.aqs[:, a:a + 128]

    def words(c, a, z):
        return c[:, a:z].bitcast(dt.uint8)

    def gather(q, out, win, offs, reads, key, after=()):
        if q == "v":
            V(lambda: v.tensor_copy(out, win.indirect(offs)), reads, [key], after=after)
        else:
            S(lambda: s.activation(out, win.indirect(offs), Act.Copy), reads, [key], after=after)

    def hop(out, in_, sem, dst, keys):
        rid, pid = topo.addr(dst, core)
        engines[0] += len(topo.engines(core, dst))
        G(lambda: g.remote_dma(out, in_, T.sem[sem], T.sem.sent, pid, rid, topo.mask(core, dst)), keys, dma="remote")

    nxt = T.cores[(rank + 1) % n]
    before = len(topo.engines(T.cores[(rank - 1) % n], core))
    home = len(topo.engines(T.cores[(rank + VISITS - 1) % n], core))

    def scaled(q, out, in_, name, key):
        if q == "s":
            S(act(out, in_, 0.015625), [name], [key])
        else:
            V(ts(out, in_, 0.015625, None, Alu.mult), [name], [key])

    def bits(c, sc, keys, a, z, pa):
        P(mm(T[pa][:, 0:z - a], T.uq[:], T.usq[:], c, sc, True, True), keys + ["uq"], [pa])
        V(ts(T.wk[:, a:z], T[pa][:, 0:z - a], 0.0, pw, Alu.is_gt, Alu.mult), [pa, "pw"], ["bits%d" % h for h in range(a // H, z // H)])

    def sums(*which):
        V(qz(T.aq[:, 0:128], T.aqs[:, 0:128], T.wk[:, 0:512]), ["bits0", "bits1"] + fls[:4], ["bitq", "flq0"])
        for j in which:
            name = ("po", "pc")[j]
            P(mm(T[name][:, 0:128], *kside(j), *work(0), True, True), ["kq%d" % j, "bitq", "flq0"], [name])

    def send_addresses(t):
        name = "rs%d" % t
        V(scan(T.v1[:], T.pc[:, 0:64], 64), ["kscan", "pc"], ["v1"])
        V(ts(T[name][:], T.v1[:, 3:64:4], scol4, None, Alu.mult), ["v1", "scol4"], [name])
        hop(T["ra%d" % t][:], T[name][:], "ar%d" % t, nxt, [name])

    def owns():
        S(act(T.own0[:], T.po[:, 0:64], bias=ge), ["po", "ge"], ["own0"])
        S(act(T.own[:], T.po[:, 0:64]), ["po"], ["own"])

    def slots(t):
        if t:
            owns()
        for j in range(SHIFTS):
            a = C + 256 * (j // 4)
            o = "own" if j else "own0"
            V(lambda j=j, a=a, o=o: v.tensor_tensor(T.wk[:, a + 4 * j + j % 4:a + 256:4], T.pc[:, 0:64 - j], T[o][:, j:64], Alu.is_equal), ["pc", o], ["fl%d" % j])
        V(qz(T.aq[:, 64:192], T.aqs[:, 64:192], T.wk[:, C:768]), fls, ["flq0", "flq1"])
        P(mm(T.ps[:, 0:128], *kside(1), *work(0), True, False), ["kq1", "bitq", "flq0"], ["ps"])
        P(mm(T.ps[:, 0:128], *kside(2), *work(64), False, False), ["kq1", "flq0", "flq1"], ["ps"])
        P(mm(T.ps[:, 0:128], *kside(2), *work(128), False, True), ["kq1", "flq1", "state0"], ["ps"])
        V(scan(T.v2[:], T.ps[:, 0:64], 64), ["kscan", "ps"], ["v2"])
        name = "os%d" % t if t else "oa0"
        for h in range(2):
            V(ts(T[name][:, h:16:2], T.v2[:, 3 + 4 * h:64:8], scol4, T.spare[:, h:h + 1], Alu.mult, Alu.min), ["v2", "scol4", "spare"], [name + "ab"[h]])
        if t:
            hop(T["oa%d" % t][:], T[name][:], "ao%d" % t, nxt, [name + "a", name + "b"])

    for t in range(VISITS):
        yc, ys = T["y%dc" % t], T["y%ds" % t]
        final = t + 1 == VISITS
        lo = 4 * M + 4 * C * t
        pk = ["pool_m"] + ["pool%d_%d%s" % (a, b, x) for a in range(t) for b in range(4) for x in ("", "x")]
        yq = ["yq%d0" % t, "yq%d1" % t]
        dst = T.cores[(rank - VISITS + 1) % n] if final else nxt
        land = T["l%dc" % (t + 1)]

        if t == 0:
            bits(T.aq[:, 192:192 + C], T.aqs[:, 192:192 + C], ["state0"], 0, C, "pa")
            sums(0, 1)
            V(ts(T.off[:], T.po[:, 0:64], bcol, None, Alu.add), ["po", "cf"], ["off0", "off1"])
            owns()
        for h in range(2):
            a, z, gv = H * h, H * h + H, GV[t][h]
            if t:
                gather(LOOK[t][h], T.look[:, a:z], T.tab[:, 0:M], T["ra%d" % t][:, 8 * h:8 * h + 8], ["tab", "tabb"], "look%d" % h, after=[("ar%d" % t, before)])
                V(scan(T.scan[:, a:z], T.look[:, a:z], H), ["kscan", "look%d" % h], ["scan%d" % h])
                V(ts(T.off[:, 32 * h:32 * h + 32], T.scan[:, a + 3:z:4], scol, bcol, Alu.mult, Alu.add), ["scan%d" % h, "scol", "cf"], ["off%d" % h])
            gather("s", T.bt[:, 4 * a + 16 * gv:4 * z], T.pool[:, 0:lo], T.off[:, 32 * h + gv:32 * h + 32], pk + ["off%d" % h], "bts%d" % h)
            gather("v", T.bt[:, 4 * a:4 * a + 16 * gv], T.pool[:, 0:lo], T.off[:, 32 * h:32 * h + gv], pk + ["off%d" % h], "btv%d" % h)
            V(qz(T.bq[:, a:z], T.bs[:, a:z], T.bt[:, 4 * a:4 * z]), ["bts%d" % h, "btv%d" % h], ["bq%d" % h])
            for b in range(4):
                name = (SETS[0], BANKS[t])[h][b]
                if t:
                    P(mm(T[name][:, 0:H], *wside(b), T["l%dc" % t][:, a:z], T["l%ds" % t][:, a:z], True, False), ["w%d" % b, "ws"], [name],
                      after=[("arr%d" % t, before), ("arc%d%d" % (t, h), before)])
                else:
                    P(mm(T[name][:, 0:H], *wside(b), T.aq[:, 192 + a:192 + z], T.aqs[:, 192 + a:192 + z], True, False), ["state0", "w%d" % b, "ws"], [name])
                P(mm(T[name][:, 0:H], *eside(b), T.bq[:, a:z], T.bs[:, a:z], False, True), ["bq%d" % h, "eq%d" % b], [name])
                scaled(COPY[t][h][b], T.yt[:, 4 * a + b:4 * z:4], T[name][:, 0:H], name, "yt%d%d" % (h, b))
            V(qz(yc[:, a:z], ys[:, a:z], T.yt[:, 4 * a:4 * z]), ["yt%d%d" % (h, b) for b in range(4)], [yq[h]])
        if t == 0:
            slots(0)
        for h in range(2):
            hop(words(land, H * h, H * h + H), words(yc, H * h, H * h + H), "arc%d%d" % (t + 1, h), dst, [yq[h]])
        hop(T.fins[:, 0:C] if final else T["l%ds" % (t + 1)][:], ys[:], "arr%d" % (t + 1), dst, yq)
        if not final:
            bits(yc[:, 0:H], ys[:, 0:H], yq[:1], 0, H, ABANK[t])
            bits(yc[:, H:C], ys[:, H:C], yq[1:], H, C, "pa")
            sums(1, 0)
            send_addresses(t + 1)
        for h, (a, z) in enumerate(((0, H), (H, C)) if len(WRITE[t]) == 8 else ((0, C),)):
            for b in range(4):
                name = SETS[h if final else 0][(b + 2) % 4]
                P(mm(T[name][:, 0:z - a], *eside(b), yc[:, a:z], ys[:, a:z], True, True), yq[a // H:z // H] + ["eq%d" % b], [name])
                scaled(WRITE[t][4 * h + b], T.pool[:, lo + 4 * a + b:lo + 4 * z:4], T[name][:, 0:z - a], name, "pool%d_%d%s" % (t, b, "x" * h))
        for k in range(7, -1, -1):
            V(lambda k=k, t=t: v.tensor_copy(T.tab[:].indirect(T["oa%d" % t][:, 2 * k:2 * k + 2]), T.val[:, C * t + 32 * k:C * t + 32 * k + 32]),
              ["oa0a", "oa0b", "val%d" % t], ["tab", "tabb"], after=[("ao%d" % t, before)] if t else [])
        if not final:
            slots(t + 1)

    pk = pk + ["pool%d_%d%s" % (VISITS - 1, b, x) for b in range(4) for x in ("", "x")]
    for a, z, share in LAST:
        key = str(a)
        V(scan(T.mscan[:, 4 * a:4 * z], T.tab[:, 4 * a:4 * z], 4 * (z - a)), ["kscan", "tab", "tabb"], ["mscan" + key])
        V(ts(T.moff[:, a:z], T.mscan[:, 4 * a + 3:4 * z:4], scol, bcol, Alu.mult, Alu.add), ["mscan" + key, "scol", "cf"], ["moff" + key])
        gather("s", T.mc[:, 16 * a:16 * (a + share)], T.pool[:], T.moff[:, a:a + share], pk + ["moff" + key], "ms" + key)
        gather("v", T.mc[:, 16 * (a + share):16 * z], T.pool[:], T.moff[:, a + share:z], pk + ["moff" + key], "mv" + key)
        V(qz(T.qmc[:, 4 * a:4 * z], T.fins[:, C + 4 * a:C + 4 * z], T.mc[:, 16 * a:16 * z]), ["ms" + key, "mv" + key], ["qm" + key])

    codes, plane = [("arc30", home), ("arc31", home)], [("arr3", home)]
    qm = ["qm%d" % a for a, z, share in LAST]
    P(mm(T.pr0[:, 0:C], *wside(0), T.l3c[:], T.fins[:, 0:C], True, True), ["w0", "ws"], ["pr0"], after=codes + plane)
    if YCOPY == "s":
        S(act(T.ysb[:], T.pr0[:, 0:C]), ["pr0"], ["ysb"])
    else:
        V(lambda: v.tensor_copy(T.ysb[:], T.pr0[:, 0:C]), ["pr0"], ["ysb"])
    load(YQ, T.y[:], T.ysb[:], ["ysb"], (), "dy")
    load(OQ[0], T.oc[:, 0:4 * C], words(T.l3c, 0, C), (), (), "dsc", after=codes)
    for h, (a, z) in enumerate(STORES):
        load(OQ[1 + h], T.oc[:, 4 * C + 16 * a:4 * C + 16 * z], words(T.qmc, 4 * a, 4 * z), ["qm%d" % a2 for a2, z2, share in LAST if a <= a2 < z], (), "dm%d" % h)
    for k in range(4):
        load(SQ[k], T.osc[4 * k:4 * k + 4, :], T.fins[32 * k:32 * k + 4, :], qm, (), "ds%d" % k, after=plane)

    order = ORDER or list(range(len(ops)))
    place = {d: i for i, d in enumerate(order)}
    last = {}
    for me in order:
        o, best = ops[me], {}
        for d in o["deps"]:
            key = ops[d]["dma"] or ops[d]["q"]
            if key not in best or place[best[key]] < place[d]:
                best[key] = d
        o["deps"] = []
        for key, d in best.items():
            if last.get((o["q"], key), -1) < place[d]:
                last[(o["q"], key)] = place[d]
                ops[d]["need"] = True
                o["deps"].append(d)
    count, seen = {}, set()
    for me in order:
        o = ops[me]
        q = o["q"]
        for name, val in o["after"]:
            if (q, name) not in seen:
                seen.add((q, name))
                eng[q].wait_ge(T.sem[name], val)
        for d in o["deps"]:
            eng[q].wait_ge(T.sem[ops[d]["sem"]], ops[d]["val"])
        ins = o["fn"]()
        if o["dma"] == "remote":
            continue
        if o["dma"]:
            o["sem"], o["val"] = o["dma"], 16
            ins.then_inc(T.sem[o["dma"]], 16)
        elif o["need"]:
            count[q] = count.get(q, 0) + 1
            o["sem"], o["val"] = counter[q], count[q]
            ins.then_inc(T.sem[counter[q]], 1)
    g.wait_ge(T.sem.sent, engines[0])
    for o in ops:
        if o["dma"] not in (None, "remote") and not o["need"]:
            eng[o["q"]].wait_ge(T.sem[o["dma"]], 16)
